import numpy as np, ml_dtypes
CORES = [2,3,42,43,82,83,122,123]
N = 8
import mx_ref
BF = ml_dtypes.bfloat16
def entries(a):
    return np.ascontiguousarray(a.T).reshape(-1)
def table(e):
    return np.ascontiguousarray(np.reshape(e, (-1, 16)).T).astype(np.int32)
def pick(q, e):
    c = np.concatenate([q[0].reshape(128, -1, 4), np.zeros((128, 1, 4), np.uint8)], axis=1); s = np.concatenate([q[1], np.ones((16, 1), np.uint8)], axis=1)
    return (np.ascontiguousarray(c[:, e].reshape(128, -1)), np.ascontiguousarray(s[:, e]))
def join(*qs):
    return (np.concatenate([q[0] for q in qs], axis=1), np.concatenate([q[1] for q in qs], axis=1))
def put(q, e, v):
    c, s = q[0].reshape(128, -1, 4).copy(), q[1].copy(); c[:, e] = v[0].reshape(128, -1, 4); s[:, e] = v[1]
    return (c.reshape(128, -1), s)
def pk(c, s):
    return (np.ascontiguousarray(c), mx_ref.live(s))
def emit(q):
    return q[0], q[1]
def packed(v, rng):
    q = [mx_ref.quantize(np.ascontiguousarray(v[r])) for r in range(N)]
    return np.stack([a for a, b in q]), np.stack([mx_ref.plane(b, rng) for a, b in q])
def cols(t, e):
    v = np.concatenate([t.reshape(128, -1, 4), np.zeros((128, 1, 4), BF)], axis=1)
    return np.ascontiguousarray(v[:, e]).reshape(128, -1)
def f(rng, *shape):
    return mx_ref.flush((rng.standard_normal(shape, dtype=np.float32) * np.exp2(rng.integers(-2, 3, shape[:-1] + (1,)))).astype(BF))
def wide(rng, *shape, cols=0):
    v = rng.standard_normal(shape, dtype=np.float32) * np.exp2(rng.integers(-12, 13, shape)).astype(np.float32)
    if cols: v *= np.repeat(np.exp2(rng.integers(-cols, cols + 1, shape[:-2] + (1, shape[-1] // 4))) * (rng.random(shape[:-2] + (1, shape[-1] // 4)) > 0.0625), 4, axis=-1).astype(np.float32)
    return mx_ref.flush(v.astype(BF))
T, C, CAPP, M = 256, 512, 32, 128
def first(v):
    z = np.zeros((N, 128, 512), BF); z[:, :, :4] = v; return z
def lists(rng, full=False, one=False, odd=False):
    h = int(rng.integers(0, N)); a = rng.permutation(np.delete(np.arange(N), h))
    sn = np.full((N, N, CAPP), -1)
    for d in range(N):
        m, o = int(rng.integers(1, M + 1)), rng.permutation(N * CAPP)
        if odd: m = 2 * int(rng.integers(0, M // 2)) + 1
        if full:
            w = np.isin(o // CAPP, a[:M // CAPP] if d == h else a[:1]); o = np.concatenate([o[w], o[~w]])
            m = M if d == h else int(rng.integers(CAPP, M + 1))
        if one: o = o[o // CAPP != a[0]]
        if one and d == h: m, o = 1, o[o // CAPP != h]
        o = o[:m]
        sn[o // CAPP, d, o % CAPP] = rng.integers(0, T, m)
    return np.stack([table(sn[s]) for s in range(N)])
def setup_inputs(rng):
    kc, ks = packed(f(rng, N, 128, 4 * C), rng)
    return {"x": f(rng, N, 128, 4 * T), "u": first(f(rng, N, 128, 4)), "w": f(rng, N, 128, 512), "kc": kc, "ks": ks, "sn": lists(rng)}
def setup_inputs_full(rng):
    return {**setup_inputs(rng), "sn": lists(rng, full=True)}
def setup_inputs_high(rng):
    d = setup_inputs(rng); g = np.where(rng.permutation(N) < N // 2, 1, -1).astype(np.float32)[:, None, None]
    p = rng.permutation(N)
    g = g * np.where(p < N // 2, 2.0 ** 24, 2.0 ** -24).astype(np.float32)[:, None, None]
    k = np.where(p == N - 1, 2.0 ** -24, 2.0 ** 24).astype(np.float32)[:, None, None]
    d["u"] = first(((np.abs(f(rng, N, 128, 4).astype(np.float32)) + 1) * k).astype(BF))
    d["kc"], d["ks"] = packed((g * (1 + np.abs(f(rng, N, 128, 4 * C).astype(np.float32)))).astype(BF), rng); return d
def setup_inputs_one(rng):
    return {**setup_inputs(rng), "sn": lists(rng, one=True)}
def setup_inputs_spread(rng):
    d = setup_inputs(rng); d["x"] = wide(rng, N, 128, 4 * T, cols=8)
    d["kc"], d["ks"] = packed(wide(rng, N, 128, 4 * C, cols=8), rng); return d
def setup_inputs_ties(rng):
    d = setup_inputs(rng); v = f(rng, N, 128, C // 8 * 4)
    d["kc"], d["ks"] = packed(np.stack([cols(v[r], rng.permutation(np.arange(C) // 8)) for r in range(N)]), rng)
    d["u"][int(rng.integers(0, N))] = 0
    d["sn"] = lists(rng, odd=True); return d
def scores(u, kc, ks):
    return mx_ref.matmul(mx_ref.quantize(np.ascontiguousarray(u)), pk(kc, ks))[0] + np.float32(0)
def check_inputs(d):
    b = []
    for r in range(N):
        if (d["u"][r][:, 4:].astype(np.float32) != 0).any(): b.append("u")
        e = entries(d["sn"][r])
        m = sum(int((entries(d["sn"][s])[r * CAPP:r * CAPP + CAPP] >= 0).sum()) for s in range(N))
        if e.min() < -1 or e.max() >= T or m < 1 or m > M: b.append("sn")
        try: good = bool(np.isfinite(scores(d["u"][r], d["kc"][r], d["ks"][r])).all())
        except Exception: good = False
        if not good: b.append("kc")
    return b
def reference(x, u, w, kc, ks, sn):
    oc, osc, ev = np.zeros((N, 128, 4 * C), np.uint8), np.zeros((N, 16, C), np.uint8), np.zeros((N, 2, M), np.float32)
    y = np.zeros((N, 128, C), np.float32)
    new = join(*[mx_ref.quantize(np.ascontiguousarray(x[s])) for s in range(N)])
    for d in range(N):
        e = []
        for s in range(N):
            v = entries(sn[s])[d * CAPP:d * CAPP + CAPP]; e.append(s * T + v[v >= 0])
        e = np.concatenate(e); m = e.size
        z = scores(u[d], kc[d], ks[d])
        out = np.argsort(z, kind="stable")[:m]
        after = put(pk(kc[d], ks[d]), out, pick(new, e))
        oc[d], osc[d] = emit(after)
        ev[d, 0] = -1; ev[d, 0, :m] = out; ev[d, 1, :m] = z[out]
        y[d] = mx_ref.matmul(mx_ref.quantize(np.ascontiguousarray(w[d])), after)
    return {"oc": oc, "osc": osc, "ev": ev, "y": y}

@@ -1,0 +1,336 @@
+from concourse.bass import DstId, RemoteDMATransfer
+from concourse.mybir import dt, AluOpType as A, ActivationFunctionType as F
+
+N, CAPP, C, M = 8, 32, 512, 128
+NS = N * CAPP
+X4, U8, F32, BF, I32, U16 = "float8_e4m3fn_x4", "uint8", "float32", "bfloat16", "int32", "uint16"
+
+
+def _sb(n, d):
+    return ("sbuf", [128, n], d)
+
+
+SCRATCH = {
+    "snr": _sb(16, I32), "snoff": _sb(16, U16), "va": _sb(8, F32), "vb": _sb(8, F32), "vf": _sb(8, F32),
+    "xt": _sb(1024, BF), "xq": _sb(256, X4), "xs": _sb(256, U8),
+    "slq": _sb(256, X4), "sls": _sb(256, U8),
+    "cand": _sb(NS + C, X4), "cands": _sb(NS + C, U8), "aft": _sb(512, X4), "afts": _sb(512, U8),
+    "uw": _sb(4, BF), "ut": _sb(512, BF), "uq": _sb(128, X4), "us": _sb(128, U8),
+    "wt": _sb(512, BF), "wq": _sb(128, X4), "ws": _sb(128, U8),
+    "p4i": _sb(32, I32), "p4j": _sb(32, I32), "off4": _sb(32, U16),
+    "pidx": _sb(2, I32), "hbit": _sb(2, I32), "hm": _sb(1, F32), "hn": _sb(1, F32),
+    "mu": _sb(128, F32), "ones": _sb(32, BF), "zr": _sb(NS, BF), "j2": _sb(4, F32),
+    "lv": _sb(8, F32), "bc": _sb(256, BF), "vrow": _sb(256, BF), "pre": _sb(256, F32),
+    "sv": _sb(4, F32), "dl": _sb(4, F32), "xx": _sb(512, F32), "cm": _sb(2048, BF), "scl": _sb(1024, BF), "jk": _sb(1024, BF),
+    "ke": _sb(4, F32), "g8": _sb(8, F32), "w8": _sb(8, F32), "ab": _sb(16, F32), "zb": _sb(32, F32), "zt": _sb(32, F32),
+    "bt": _sb(64, F32), "wl": _sb(64, F32), "foff": _sb(32, U16), "eoff": _sb(16, U16),
+    "evin": _sb(256, F32), "evw": _sb(1024, F32), "evs": _sb(128, F32), "evo": _sb(128, F32), "ysb": _sb(512, F32),
+    "ra": ("psum", [128, 512], F32), "rc": ("psum", [128, 512], F32), "sa": ("psum", [128, 512], F32), "sc": ("psum", [128, 512], F32),
+    "pc0": ("psum", [128, 512], F32), "pc1": ("psum", [128, 512], F32), "pc2": ("psum", [128, 512], F32), "pc3": ("psum", [128, 512], F32),
+}
+SEMAPHORES = ["v", "s", "t", "gq", "d_sn", "d_x", "d_u", "d_k0", "d_k1", "d_w", "d_ev", "d_out", "larr", "arrc", "arrs", "loc"]
+
+
+def _deal(dst, engs):
+    r, k = {}, 0
+    two = len(engs) - len(dst)
+    for n, d in enumerate(dst):
+        w = 2 if n >= len(dst) - two else 1
+        r[d] = engs[k:k + w]
+        k += w
+    return r
+
+
+def _engines(T, topo, s):
+    me = T.cores[s]
+    rest = [(s + k) % N for k in range(1, N)]
+    on = [d for d in rest if topo.chip(T.cores[d]) == topo.chip(me)]
+    off = [d for d in rest if topo.chip(T.cores[d]) != topo.chip(me)]
+    e_off = topo.engines(me, T.cores[off[0]])
+    e_on = [e for e in topo.engines(me, T.cores[on[0]]) if e not in e_off]
+    h = len(e_off) // 2
+    a = _deal(off, e_off)
+    b = _deal(off[2:] + off[:2], e_off[h:] + e_off[:h])
+    a[on[0]] = b[on[0]] = e_on[:len(e_on) // 4]
+    return a, b
+
+
+def rank_program(g, core, T, topo):
+    r = T.rank_of(core)
+    if r is None:
+        return
+    sem = T.sem
+    cnt = {"v": 0, "s": 0, "t": 0, "gq": 0}
+    seen = {}
+    qs = {"v": g.vector, "s": g.scalar, "t": g.tensor, "gq": g, "y": g.sync}
+
+    def need(q, *deps):
+        for name, val in deps:
+            if seen.get((q, name), 0) < val:
+                qs[q].wait_ge(sem[name], val)
+                seen[(q, name)] = val
+
+    def done(q, ins):
+        ins.then_inc(sem[q], 1)
+        cnt[q] += 1
+        return (q, cnt[q])
+
+    V, S, Y = g.vector, g.scalar, g.sync
+    dma = {}
+
+    def load(q, name, out, in_):
+        q.dma_start(out, in_).then_inc(sem[name], 16)
+        dma[name] = dma.get(name, 0) + 16
+        return (name, dma[name])
+
+    for k in range(4):
+        load(Y, "d_sn", T.snr[16 * k:16 * k + 16, :], T.sn[:])
+        d_sn = load(S, "d_sn", T.snr[64 + 16 * k:80 + 16 * k, :], T.sn[:])
+    d_u = load(S, "d_u", T.uw[:], T.u[:, 0:4])
+    d_x = load(Y, "d_x", T.xt[:], T.x[:])
+    d_k = []
+    for k in range(2):
+        a, b = 256 * k, 256 * k + 256
+        load(Y, "d_k%d" % k, T.cand[:, NS + a:NS + b].bitcast(dt.uint8), T.kc[:, 4 * a:4 * b])
+        d_k.append(load(Y, "d_k%d" % k, T.cands[:, NS + a:NS + b], T.ks[:, a:b]))
+    d_w = load(Y, "d_w", T.wt[:], T.w[:])
+
+    g_p4 = done("gq", g.iota(T.p4i[:], [[0, 32]], 0, 1))
+    g_pi = done("gq", g.iota(T.pidx[:], [[0, 2]], 0, 1))
+    v_mu = done("v", V.memset(T.mu[:], 1.0))
+    v_one = done("v", V.memset(T.ones[:], 1.0))
+    need("v", g_p4)
+    a = done("v", V.tensor_scalar(T.p4j[:], T.p4i[:], 3, None, A.bitwise_and))
+    need("v", g_pi)
+    b = done("v", V.tensor_scalar(T.hbit[:], T.pidx[:], 4, 1, A.arith_shift_right, A.bitwise_and))
+    need("v", a)
+    v_off4 = done("v", V.tensor_copy(T.off4[:], T.p4j[:]))
+    need("v", b)
+    v_hm = done("v", V.tensor_copy(T.hm[:], T.hbit[:, 0:1]))
+    need("v", v_hm)
+    v_hn = done("v", V.tensor_scalar(T.hn[:], T.hm[:], -1.0, 1.0, A.mult, A.add))
+    need("gq", v_mu)
+    g_mu = done("gq", g.affine_select(T.mu[:], T.mu[:], [[-1, 128]], A.is_gt, 0.0, 0, 1))
+    g_j2 = done("gq", g.iota(T.j2[:], [[256, 4]], 0, 2, allow_small_or_imprecise_dtypes=True))
+    done("v", V.memset(T.w8[:, 4:8], 0.0))
+    v_zr = done("v", V.memset(T.zr[:], 0.0))
+
+    need("v", d_sn, v_hn)
+    a = done("v", V.tensor_scalar(T.va[:], T.snr[:, 0:16:2], 0.0, T.hn[:], A.is_ge, A.mult))
+    b = done("v", V.tensor_scalar(T.vb[:], T.snr[:, 1:16:2], 0.0, T.hm[:], A.is_ge, A.mult))
+    v_sno = done("v", V.tensor_copy(T.snoff[:], T.snr[:]))
+    need("v", b)
+    v_vf = done("v", V.tensor_tensor(T.vf[:], T.va[:], T.vb[:], A.add))
+
+    need("s", v_off4, d_u)
+    s_ut = done("s", S.activation(T.ut[:], T.uw[:].indirect(T.off4[:]), F.Copy))
+    a = done("v", V.memset(T.evw[:, 0:M], 0.0))
+    need("v", a)
+    v_evw = done("v", V.memset(T.evw[0:32, 0:M], -1.0))
+    need("v", s_ut)
+    v_uq = done("v", V.quantize_mx(T.uq[:], T.us[:], T.ut[:]))
+
+    need("v", d_x)
+    v_xq = done("v", V.quantize_mx(T.xq[:], T.xs[:], T.xt[:]))
+    need("v", v_xq, v_sno)
+    v_sl = done("v", V.tensor_copy(T.slq[:].bitcast(dt.uint32), T.xq[:].bitcast(dt.uint32).indirect(T.snoff[:, 0:16])))
+    o = CAPP * r
+    v_own = done("v", V.tensor_copy(T.cand[:, o:o + CAPP].bitcast(dt.uint32),
+                                    T.xq[:].bitcast(dt.uint32).indirect(T.snoff[:, 2 * r:2 * r + 2])))
+    need("s", v_xq, v_sno)
+    s_sl = done("s", S.activation(T.sls[:], T.xs[:].indirect(T.snoff[:, 0:16]), F.Copy))
+    s_own = done("s", S.activation(T.cands[:, o:o + CAPP], T.xs[:].indirect(T.snoff[:, 2 * r:2 * r + 2]), F.Copy))
+
+    local = [0]
+
+    def send(engs, src, dst, rs):
+        tr = []
+        for d, es in engs.items():
+            rid, pid, _ = topo.addr(T.cores[d])
+            m = 0
+            for e in es:
+                m |= 1 << e
+            tr.append(RemoteDMATransfer(dst_ids=[DstId(rid=rid, pnc=pid)], dma_engine_mask=m, remote_sem=sem[rs],
+                                        srcs=[src(d)], dsts=[dst]))
+            local[0] += len(es)
+        g.remote_dma_fused(tr, local_sem=sem["loc"])
+
+    ec, es = _engines(T, topo, r)
+    need("gq", v_vf)
+    send(ec, lambda d: T.vf[:, d:d + 1], T.lv[:, r:r + 1], "larr")
+    need("gq", v_sl)
+    send(ec, lambda d: T.slq[:, CAPP * d:CAPP * d + CAPP].bitcast(dt.uint8), T.cand[:, o:o + CAPP].bitcast(dt.uint8), "arrc")
+    need("gq", s_sl)
+    send(es, lambda d: T.sls[:, CAPP * d:CAPP * d + CAPP], T.cands[:, o:o + CAPP], "arrs")
+    nc = sum(len(_engines(T, topo, s)[0][r]) for s in range(N) if s != r)
+    nl = sum(len(_engines(T, topo, s)[1][r]) for s in range(N) if s != r)
+    larr, arrc, arrs = ("larr", nc), ("arrc", nc), ("arrs", nl)
+    need("gq", g_j2)
+    g_ev = done("gq", g.iota(T.evin[0:32, :], [[1, 256]], 0, 0, allow_small_or_imprecise_dtypes=True))
+    need("gq", g_ev)
+    g_ev = done("gq", g.iota(T.evin[64:96, :], [[1, 256]], 257, 0, allow_small_or_imprecise_dtypes=True))
+
+    need("t", v_uq)
+    t_pc, t_r, t_s = [], [], []
+
+    def row(nm, h):
+        a = NS + 256 * h
+        return done("t", g.tensor.matmul_mx(T[nm + "ac"[h]][:, 0:256], T.uq[:], T.us[:], T.cand[:, a:a + 256],
+                                            T.cands[:, a:a + 256], True, True))
+
+    for h in range(2):
+        need("t", d_k[h])
+        for k in (2 * h, 2 * h + 1):
+            a = NS + 128 * k
+            t_pc.append(done("t", g.tensor.matmul_mx(T["pc%d" % k][:, 0:128], T.cand[:, a:a + 128], T.cands[:, a:a + 128],
+                                                     T.uq[:], T.us[:], True, True)))
+        t_r.append(row("r", h))
+    for h in range(2):
+        t_s.append(row("s", h))
+
+    v_sv = {}
+    for k in range(2):
+        need("v", t_pc[k])
+        v_sv[k] = done("v", V.tensor_copy(T.sv[:, k:k + 1], T["pc%d" % k][:, 0:1]))
+    s_x = {}
+
+    def thresholds(h):
+        need("s", v_sv[2 * h], v_sv[2 * h + 1], g_mu)
+        a = done("s", S.activation(T.dl[:, 2 * h:2 * h + 2], T.sv[:, 2 * h:2 * h + 2], F.Abs, scale=0.74 * 2.0 ** -23, bias=2e-38))
+        need("s", a)
+        for k in (2 * h, 2 * h + 1):
+            s_x[k] = done("s", S.activation(T.xx[:, 128 * k:128 * k + 128], T.mu[:], F.Identity, bias=T.sv[:, k:k + 1], scale=T.dl[:, k:k + 1]))
+
+    thresholds(0)
+    for k in range(2, 4):
+        need("s", t_pc[k])
+        v_sv[k] = done("s", S.activation(T.sv[:, k:k + 1], T["pc%d" % k][:, 0:1], F.Copy))
+    thresholds(1)
+    need("s", larr, v_one, v_vf)
+    for s in range(N):
+        col = T.vf[:, r:r + 1] if s == r else T.lv[:, s:s + 1]
+        s_bc = done("s", S.activation(T.bc[:, CAPP * s:CAPP * s + CAPP], T.ones[:], F.Copy, scale=col))
+    for h in range(2):
+        need("s", t_s[h])
+        s_ev = done("s", S.activation(T.evin[32 + 64 * h:64 + 64 * h, :], T["s" + "ac"[h]][32 + 64 * h:64 + 64 * h, 0:256], F.Copy))
+
+    v_cm, v_sc = {}, {}
+
+    def outer(k, h, lo, hi, op):
+        need("v", t_r[h], v_sv[k])
+        v_cm[k] = done("v", V.tensor_scalar(T.cm[:, 512 * k + 256 * h + lo:512 * k + 256 * h + hi], T["r" + "ac"[h]][:, lo:hi],
+                                            T.sv[:, k:k + 1], None, op))
+
+    def inner(k):
+        a = 128 * (k % 2)
+        need("v", s_x[k], t_r[k // 2])
+        v_cm[k] = done("v", V.tensor_tensor(T.cm[:, 640 * k:640 * k + 128], T["r" + "ac"[k // 2]][:, a:a + 128],
+                                            T.xx[:, 128 * k:128 * k + 128], A.is_lt))
+
+    def total(k):
+        need("v", v_cm[k])
+        v_sc[k] = done("v", V.tensor_tensor_scan(T.scl[:, 256 * k:256 * k + 256], T.cm[:, 512 * k:512 * k + 256],
+                                                 T.cm[:, 512 * k + 256:512 * k + 512], -256.0, A.add, A.add))
+
+    def stay(k):
+        need("v", v_sc[k], v_pre, g_j2)
+        return done("v", V.tensor_scalar(T.w8[:, k:k + 1], T.scl[:, 256 * k + 255:256 * k + 256], T.pre[:, 255:256],
+                                         T.j2[:, k:k + 1], A.is_ge, A.mult))
+
+    outer(1, 0, 0, 128, A.is_le)
+    outer(0, 0, 128, 256, A.is_lt)
+    inner(0)
+    inner(1)
+    outer(2, 0, 0, 256, A.is_le)
+    outer(3, 0, 0, 256, A.is_le)
+    outer(0, 1, 0, 256, A.is_lt)
+    outer(1, 1, 0, 256, A.is_lt)
+    total(0)
+    need("v", s_bc)
+    v_vr = done("v", V.transpose(T.vrow[:], T.bc[:]))
+    total(1)
+    need("v", v_vr, v_zr)
+    v_pre = done("v", V.tensor_tensor_scan(T.pre[:], T.vrow[:], T.zr[:], -256.5, A.add, A.add))
+    outer(2, 1, 128, 256, A.is_lt)
+    inner(2)
+    stay(0)
+    outer(3, 1, 0, 128, A.is_le)
+    total(2)
+    inner(3)
+    stay(1)
+    total(3)
+    stay(2)
+    for k in range(4):
+        need("s", v_pre, v_sc[k])
+        s_acc = done("s", S.activation(T.jk[:, 256 * k:256 * k + 256], T.pre[:], F.Sign, bias=T.scl[:, 256 * k + 255:256 * k + 256],
+                                       scale=-1.0, accum_out=T.g8[:, k:k + 1]))
+    v_w8 = stay(3)
+    v_ke = done("v", V.tensor_scalar(T.ke[:], T.scl[:, 255:1024:256], T.pre[:, 255:256], 512.0, A.is_ge, A.mult))
+    need("v", d_w)
+    v_wq = done("v", V.quantize_mx(T.wq[:], T.ws[:], T.wt[:]))
+    need("v", v_ke)
+    v_e = done("v", V.tensor_tensor(T.g8[:, 4:8], T.ke[:], T.scl[:, 255:1024:256], A.add))
+
+    need("v", s_acc, v_w8, v_e)
+    for c in range(2):
+        for h in range(2):
+            v_ab = done("v", V.tensor_tensor(T.ab[64 * h:64 * h + 64, c:16:2], T.g8[64 * c:64 * c + 64, :], T.w8[64 * c:64 * c + 64, :], A.add))
+    need("v", v_ab)
+    need("s", v_ab)
+    for q in range(2):
+        for c in range(2):
+            a, b = 32 * q, 32 * c
+            v_zb = done("v", V.tensor_copy(T.zb[a:a + 32, c:32:2], T.ab[b:b + 32, :]))
+            s_zb = done("s", S.activation(T.zb[64 + a:96 + a, c:32:2], T.ab[64 + b:96 + b, :], F.Copy))
+    need("v", v_zb, s_zb)
+    v_zt = done("v", V.transpose(T.zt[:], T.zb[:]))
+    need("v", v_zt)
+    need("s", v_zt)
+    for h in range(2):
+        v_bt = done("v", V.tensor_copy(T.bt[:, 16 * h:16 * h + 16], T.zt[:, 0:16]))
+        s_bt = done("s", S.activation(T.bt[:, 32 + 16 * h:48 + 16 * h], T.zt[:, 16:32], F.Copy))
+    need("v", v_bt, s_bt)
+    v_wl = done("v", V.transpose(T.wl[:], T.bt[:]))
+    need("v", v_wl)
+    for b in range(2):
+        v_fo = done("v", V.tensor_scalar(T.foff[:, b:32:2], T.wl[:, 32 * b:32 * b + 16], 0.5, 128.0, A.mult, A.add))
+
+    need("v", v_fo, arrc, v_own, d_k[0], d_k[1])
+    need("s", v_fo, arrs, s_own, d_k[0], d_k[1])
+    v_af, s_af, t_y = [], [], []
+    for k in range(2):
+        a, f = 256 * k, T.foff[:, 16 * k:16 * k + 16]
+        v_af.append(done("v", V.tensor_copy(T.aft[:, a:a + 256].bitcast(dt.uint32), T.cand[:].bitcast(dt.uint32).indirect(f))))
+        s_af.append(done("s", S.activation(T.afts[:, a:a + 256], T.cands[:].indirect(f), F.Copy)))
+        need("t", v_af[k], s_af[k], v_wq)
+        t_y.append(done("t", g.tensor.matmul_mx(T["pc%d" % k][:, 0:256], T.wq[:], T.ws[:], T.aft[:, a:a + 256], T.afts[:, a:a + 256], True, True)))
+        need("y", v_af[k])
+        load(Y, "d_out", T.oc[:, 4 * a:4 * a + 1024], T.aft[:, a:a + 256].bitcast(dt.uint8))
+    for k in range(2):
+        a = 256 * k
+        need("s", t_y[k])
+        s_y = done("s", S.activation(T.ysb[:, a:a + 256], T["pc%d" % k][:, 0:256], F.Copy))
+        need("s" if k else "y", s_y)
+        load(S if k else Y, "d_out", T.y[:, a:a + 256], T.ysb[:, a:a + 256])
+    for h in range(2):
+        for b in range(2):
+            c = 32 * b + 16 + 8 * h
+            v_eo = done("v", V.tensor_scalar(T.eoff[64 * h:64 * h + 64, b:16:2], T.wl[64 * h:64 * h + 64, c:c + 8], 256.0, None, A.add))
+    need("v", v_eo, s_ev, g_ev, v_evw)
+    a = done("v", V.tensor_copy(T.evw[:].indirect(T.eoff[:]), T.evin[:]))
+    need("v", a)
+    a = done("v", V.tensor_copy(T.evs[0:64, :], T.evw[64:128, 0:M]))
+    need("v", a)
+    v_ev = done("v", V.tensor_tensor(T.evo[0:64, :], T.evw[0:64, 0:M], T.evs[0:64, :], A.add))
+    need("y", s_af[1])
+    for k in range(4):
+        d_out = load(Y, "d_out", T.osc[4 * k:4 * k + 4, :], T.afts[32 * k:32 * k + 4, :])
+    need("y", v_ev)
+    need("s", v_ev)
+    load(Y, "d_ev", T.ev[0:1, :], T.evo[0:1, :])
+    d_ev = load(S, "d_ev", T.ev[1:2, :], T.evo[32:33, :])
+
+    for n, val in cnt.items():
+        need("y", (n, val))
+    need("y", d_ev, d_out)
+    need("gq", ("loc", local[0]))

@@ -11,19 +11,19 @@ def _sb(n, d):
 
 
 SCRATCH = {
-    "snr": _sb(16, I32), "snoff": _sb(16, U16), "va": _sb(8, F32), "vb": _sb(8, F32), "vf": _sb(8, F32),
+    "snr": _sb(16, I32), "snoff": _sb(16, U16), "vf": _sb(16, F32),
     "xt": _sb(1024, BF), "xq": _sb(256, X4), "xs": _sb(256, U8),
     "slq": _sb(256, X4), "sls": _sb(256, U8),
     "cand": _sb(NS + C, X4), "cands": _sb(NS + C, U8), "aft": _sb(512, X4), "afts": _sb(512, U8),
     "uw": _sb(4, BF), "ut": _sb(512, BF), "uq": _sb(128, X4), "us": _sb(128, U8),
     "wt": _sb(512, BF), "wq": _sb(128, X4), "ws": _sb(128, U8),
-    "p4i": _sb(32, I32), "p4j": _sb(32, I32), "off4": _sb(32, U16),
-    "pidx": _sb(2, I32), "hbit": _sb(2, I32), "hm": _sb(1, F32), "hn": _sb(1, F32),
-    "mu": _sb(128, F32), "ones": _sb(32, BF), "zr": _sb(NS, BF), "j2": _sb(4, F32),
-    "lv": _sb(8, F32), "bc": _sb(256, BF), "vrow": _sb(256, BF), "pre": _sb(256, F32),
+    "pi": _sb(32, I32), "p4": _sb(32, I32), "off4": _sb(32, U16), "bi": _sb(16, I32), "boff": _sb(16, U16),
+    "nn": _sb(16, I32), "nf": _sb(1, F32), "coff": _sb(4, U16),
+    "mu": _sb(128, F32), "zr": _sb(NS, BF), "j2": _sb(4, F32),
+    "lv": _sb(64, F32), "bc": _sb(256, BF), "vrow": _sb(256, BF), "pre": _sb(256, F32),
     "sv": _sb(4, F32), "dl": _sb(4, F32), "xx": _sb(512, F32), "cm": _sb(2048, BF), "scl": _sb(1024, BF), "jk": _sb(1024, BF),
-    "ke": _sb(4, F32), "g8": _sb(8, F32), "w8": _sb(8, F32), "ab": _sb(16, F32), "zb": _sb(32, F32), "zt": _sb(32, F32),
-    "bt": _sb(64, F32), "wl": _sb(64, F32), "foff": _sb(32, U16), "eoff": _sb(16, U16),
+    "ke": _sb(4, F32), "g8": _sb(8, F32), "w8": _sb(8, F32), "zz": _sb(64, F32), "zt": _sb(64, F32),
+    "foff": _sb(32, U16), "eoff": _sb(16, U16),
     "evin": _sb(256, F32), "evw": _sb(1024, F32), "evs": _sb(128, F32), "evo": _sb(128, F32), "ysb": _sb(512, F32),
     "ra": ("psum", [128, 512], F32), "rc": ("psum", [128, 512], F32), "sa": ("psum", [128, 512], F32), "sc": ("psum", [128, 512], F32),
     "pc0": ("psum", [128, 512], F32), "pc1": ("psum", [128, 512], F32), "pc2": ("psum", [128, 512], F32), "pc3": ("psum", [128, 512], F32),
@@ -83,6 +83,27 @@ def rank_program(g, core, T, topo):
         dma[name] = dma.get(name, 0) + 16
         return (name, dma[name])
 
+    def ts(out, in0, a, b, op0, op1=None, deps=()):
+        need("v", *deps)
+        if op1 is None:
+            return done("v", V.tensor_scalar(out, in0, a, None, op0))
+        return done("v", V.tensor_scalar(out, in0, a, b, op0, op1))
+
+    def tt(out, in0, in1, op, deps=()):
+        need("v", *deps)
+        return done("v", V.tensor_tensor(out, in0, in1, op))
+
+    def cp(out, in_, deps=()):
+        need("v", *deps)
+        return done("v", V.tensor_copy(out, in_))
+
+    def act(out, in_, func, deps=(), **kw):
+        need("s", *deps)
+        return done("s", S.activation(out, in_, func, **kw))
+
+    def words(ap):
+        return ap.bitcast(dt.uint32)
+
     for k in range(4):
         load(Y, "d_sn", T.snr[16 * k:16 * k + 16, :], T.sn[:])
         d_sn = load(S, "d_sn", T.snr[64 + 16 * k:80 + 16 * k, :], T.sn[:])
@@ -95,51 +116,49 @@ def rank_program(g, core, T, topo):
         d_k.append(load(Y, "d_k%d" % k, T.cands[:, NS + a:NS + b], T.ks[:, a:b]))
     d_w = load(Y, "d_w", T.wt[:], T.w[:])
 
-    g_p4 = done("gq", g.iota(T.p4i[:], [[0, 32]], 0, 1))
-    g_pi = done("gq", g.iota(T.pidx[:], [[0, 2]], 0, 1))
+    SH, AND = A.arith_shift_right, A.bitwise_and
+    g_pi = done("gq", g.iota(T.pi[:], [[128, 8], [0, 4]], 0, 1))
     v_mu = done("v", V.memset(T.mu[:], 1.0))
-    v_one = done("v", V.memset(T.ones[:], 1.0))
-    need("v", g_p4)
-    a = done("v", V.tensor_scalar(T.p4j[:], T.p4i[:], 3, None, A.bitwise_and))
-    need("v", g_pi)
-    b = done("v", V.tensor_scalar(T.hbit[:], T.pidx[:], 4, 1, A.arith_shift_right, A.bitwise_and))
-    need("v", a)
-    v_off4 = done("v", V.tensor_copy(T.off4[:], T.p4j[:]))
-    need("v", b)
-    v_hm = done("v", V.tensor_copy(T.hm[:], T.hbit[:, 0:1]))
-    need("v", v_hm)
-    v_hn = done("v", V.tensor_scalar(T.hn[:], T.hm[:], -1.0, 1.0, A.mult, A.add))
+    v_zr = done("v", V.memset(T.zr[:], 0.0))
+    v_ev0 = done("v", V.memset(T.evw[:, 0:M], 0.0))
     need("gq", v_mu)
     g_mu = done("gq", g.affine_select(T.mu[:], T.mu[:], [[-1, 128]], A.is_gt, 0.0, 0, 1))
     g_j2 = done("gq", g.iota(T.j2[:], [[256, 4]], 0, 2, allow_small_or_imprecise_dtypes=True))
+    p, nn = T.pi[:, 0:1], lambda k: T.nn[:, k:k + 1]
+    a4 = ts(T.p4[:], T.pi[:], 3, None, AND, deps=[g_pi])
+    ab = ts(T.bi[:], T.pi[:, 0:32:2], 4, 0x79, SH, AND)
+    n1 = ts(nn(0), p, 0x66, None, AND)
+    v_off4 = cp(T.off4[:], T.p4[:], [a4])
+    v_boff = cp(T.boff[:], T.bi[:], [ab])
+    n2 = ts(nn(1), nn(0), 15, 31, A.mult, A.add, [n1])
+    n5 = ts(nn(2), p, 34, None, A.mult)
+
+    v_vf = ts(T.vf[:], T.snr[:], 0.0, None, A.is_ge, deps=[d_sn])
+    v_sno = cp(T.snoff[:], T.snr[:])
+    v_lv = ts(T.lv[:, 8 * r:8 * r + 2], T.snr[:, 2 * r:2 * r + 2], 0.0, None, A.is_ge)
+
+    ts(nn(3), nn(1), 1, 16, SH, AND, [n2])
+    ts(nn(4), nn(1), 3, 8, SH, AND)
+    ts(nn(5), nn(2), 32, None, AND, deps=[n5])
+    a = ts(nn(6), p, 3, 1, SH, AND)
+    ts(T.nn[:, 8:10], T.pi[:, 0:8:4], 6, 2, SH, AND)
+    ts(nn(10), T.pi[:, 4:5], 5, 6, SH, AND)
     done("v", V.memset(T.w8[:, 4:8], 0.0))
-    v_zr = done("v", V.memset(T.zr[:], 0.0))
-
-    need("v", d_sn, v_hn)
-    a = done("v", V.tensor_scalar(T.va[:], T.snr[:, 0:16:2], 0.0, T.hn[:], A.is_ge, A.mult))
-    b = done("v", V.tensor_scalar(T.vb[:], T.snr[:, 1:16:2], 0.0, T.hm[:], A.is_ge, A.mult))
-    v_sno = done("v", V.tensor_copy(T.snoff[:], T.snr[:]))
-    need("v", b)
-    v_vf = done("v", V.tensor_tensor(T.vf[:], T.va[:], T.vb[:], A.add))
-
-    need("s", v_off4, d_u)
-    s_ut = done("s", S.activation(T.ut[:], T.uw[:].indirect(T.off4[:]), F.Copy))
-    a = done("v", V.memset(T.evw[:, 0:M], 0.0))
-    need("v", a)
+    a = tt(T.nn[:, 12:14], T.nn[:, 3:5], T.nn[:, 5:7], A.add, [a])
+    need("v", v_ev0)
     v_evw = done("v", V.memset(T.evw[0:32, 0:M], -1.0))
-    need("v", s_ut)
-    v_uq = done("v", V.quantize_mx(T.uq[:], T.us[:], T.ut[:]))
+    v_nf = tt(T.nf[:], nn(12), nn(13), A.add, [a])
+
+    s_ut = act(T.ut[:], T.uw[:].indirect(T.off4[:]), F.Copy, [v_off4, d_u])
 
     need("v", d_x)
     v_xq = done("v", V.quantize_mx(T.xq[:], T.xs[:], T.xt[:]))
-    need("v", v_xq, v_sno)
-    v_sl = done("v", V.tensor_copy(T.slq[:].bitcast(dt.uint32), T.xq[:].bitcast(dt.uint32).indirect(T.snoff[:, 0:16])))
+    need("v", s_ut)
+    v_uq = done("v", V.quantize_mx(T.uq[:], T.us[:], T.ut[:]))
+    v_sl = cp(words(T.slq[:]), words(T.xq[:]).indirect(T.snoff[:, 0:16]), [v_xq, v_sno])
+    v_coff = ts(T.coff[:, 0:3], T.nn[:, 8:11], T.nf[:], None, A.add, deps=[v_nf])
+    s_sl = act(T.sls[:], T.xs[:].indirect(T.snoff[:, 0:16]), F.Copy, [v_xq, v_sno])
     o = CAPP * r
-    v_own = done("v", V.tensor_copy(T.cand[:, o:o + CAPP].bitcast(dt.uint32),
-                                    T.xq[:].bitcast(dt.uint32).indirect(T.snoff[:, 2 * r:2 * r + 2])))
-    need("s", v_xq, v_sno)
-    s_sl = done("s", S.activation(T.sls[:], T.xs[:].indirect(T.snoff[:, 0:16]), F.Copy))
-    s_own = done("s", S.activation(T.cands[:, o:o + CAPP], T.xs[:].indirect(T.snoff[:, 2 * r:2 * r + 2]), F.Copy))
 
     local = [0]
 
@@ -157,7 +176,7 @@ def rank_program(g, core, T, topo):
 
     ec, es = _engines(T, topo, r)
     need("gq", v_vf)
-    send(ec, lambda d: T.vf[:, d:d + 1], T.lv[:, r:r + 1], "larr")
+    send(ec, lambda d: T.vf[:, 2 * d:2 * d + 2], T.lv[:, 8 * r:8 * r + 2], "larr")
     need("gq", v_sl)
     send(ec, lambda d: T.slq[:, CAPP * d:CAPP * d + CAPP].bitcast(dt.uint8), T.cand[:, o:o + CAPP].bitcast(dt.uint8), "arrc")
     need("gq", s_sl)
@@ -189,43 +208,35 @@ def rank_program(g, core, T, topo):
         t_s.append(row("s", h))
 
     v_sv = {}
-    for k in range(2):
-        need("v", t_pc[k])
-        v_sv[k] = done("v", V.tensor_copy(T.sv[:, k:k + 1], T["pc%d" % k][:, 0:1]))
+    for k in (1, 0):
+        v_sv[k] = cp(T.sv[:, k:k + 1], T["pc%d" % k][:, 0:1], [t_pc[k]])
     s_x = {}
 
     def thresholds(h):
-        need("s", v_sv[2 * h], v_sv[2 * h + 1], g_mu)
-        a = done("s", S.activation(T.dl[:, 2 * h:2 * h + 2], T.sv[:, 2 * h:2 * h + 2], F.Abs, scale=0.74 * 2.0 ** -23, bias=2e-38))
-        need("s", a)
+        a = act(T.dl[:, 2 * h:2 * h + 2], T.sv[:, 2 * h:2 * h + 2], F.Abs, [v_sv[2 * h], v_sv[2 * h + 1], g_mu],
+                scale=0.74 * 2.0 ** -23, bias=2e-38)
         for k in (2 * h, 2 * h + 1):
-            s_x[k] = done("s", S.activation(T.xx[:, 128 * k:128 * k + 128], T.mu[:], F.Identity, bias=T.sv[:, k:k + 1], scale=T.dl[:, k:k + 1]))
+            s_x[k] = act(T.xx[:, 128 * k:128 * k + 128], T.mu[:], F.Identity, [a], bias=T.sv[:, k:k + 1], scale=T.dl[:, k:k + 1])
 
     thresholds(0)
     for k in range(2, 4):
-        need("s", t_pc[k])
-        v_sv[k] = done("s", S.activation(T.sv[:, k:k + 1], T["pc%d" % k][:, 0:1], F.Copy))
+        v_sv[k] = act(T.sv[:, k:k + 1], T["pc%d" % k][:, 0:1], F.Copy, [t_pc[k]])
+    s_bc = act(T.bc[:], T.lv[:].indirect(T.boff[:]), F.Copy, [larr, v_lv, v_boff])
     thresholds(1)
-    need("s", larr, v_one, v_vf)
-    for s in range(N):
-        col = T.vf[:, r:r + 1] if s == r else T.lv[:, s:s + 1]
-        s_bc = done("s", S.activation(T.bc[:, CAPP * s:CAPP * s + CAPP], T.ones[:], F.Copy, scale=col))
+    s_own = act(T.cands[:, o:o + CAPP], T.xs[:].indirect(T.snoff[:, 2 * r:2 * r + 2]), F.Copy)
     for h in range(2):
-        need("s", t_s[h])
-        s_ev = done("s", S.activation(T.evin[32 + 64 * h:64 + 64 * h, :], T["s" + "ac"[h]][32 + 64 * h:64 + 64 * h, 0:256], F.Copy))
+        s_ev = act(T.evin[32 + 64 * h:64 + 64 * h, :], T["s" + "ac"[h]][32 + 64 * h:64 + 64 * h, 0:256], F.Copy, [t_s[h]])
 
     v_cm, v_sc = {}, {}
 
     def outer(k, h, lo, hi, op):
-        need("v", t_r[h], v_sv[k])
-        v_cm[k] = done("v", V.tensor_scalar(T.cm[:, 512 * k + 256 * h + lo:512 * k + 256 * h + hi], T["r" + "ac"[h]][:, lo:hi],
-                                            T.sv[:, k:k + 1], None, op))
+        v_cm[k] = ts(T.cm[:, 512 * k + 256 * h + lo:512 * k + 256 * h + hi], T["r" + "ac"[h]][:, lo:hi],
+                     T.sv[:, k:k + 1], None, op, deps=[t_r[h], v_sv[k]])
 
     def inner(k):
         a = 128 * (k % 2)
-        need("v", s_x[k], t_r[k // 2])
-        v_cm[k] = done("v", V.tensor_tensor(T.cm[:, 640 * k:640 * k + 128], T["r" + "ac"[k // 2]][:, a:a + 128],
-                                            T.xx[:, 128 * k:128 * k + 128], A.is_lt))
+        v_cm[k] = tt(T.cm[:, 640 * k:640 * k + 128], T["r" + "ac"[k // 2]][:, a:a + 128], T.xx[:, 128 * k:128 * k + 128], A.is_lt,
+                     [s_x[k], t_r[k // 2]])
 
     def total(k):
         need("v", v_cm[k])
@@ -233,19 +244,18 @@ def rank_program(g, core, T, topo):
                                                  T.cm[:, 512 * k + 256:512 * k + 512], -256.0, A.add, A.add))
 
     def stay(k):
-        need("v", v_sc[k], v_pre, g_j2)
-        return done("v", V.tensor_scalar(T.w8[:, k:k + 1], T.scl[:, 256 * k + 255:256 * k + 256], T.pre[:, 255:256],
-                                         T.j2[:, k:k + 1], A.is_ge, A.mult))
+        return ts(T.w8[:, k:k + 1], T.scl[:, 256 * k + 255:256 * k + 256], T.pre[:, 255:256], T.j2[:, k:k + 1], A.is_ge, A.mult,
+                  [v_sc[k], v_pre, g_j2])
 
     outer(1, 0, 0, 128, A.is_le)
     outer(0, 0, 128, 256, A.is_lt)
+    outer(0, 1, 0, 256, A.is_lt)
+    outer(1, 1, 0, 256, A.is_lt)
     inner(0)
     inner(1)
     outer(2, 0, 0, 256, A.is_le)
-    outer(3, 0, 0, 256, A.is_le)
-    outer(0, 1, 0, 256, A.is_lt)
-    outer(1, 1, 0, 256, A.is_lt)
     total(0)
+    outer(3, 0, 0, 256, A.is_le)
     need("v", s_bc)
     v_vr = done("v", V.transpose(T.vrow[:], T.bc[:]))
     total(1)
@@ -261,67 +271,51 @@ def rank_program(g, core, T, topo):
     total(3)
     stay(2)
     for k in range(4):
-        need("s", v_pre, v_sc[k])
-        s_acc = done("s", S.activation(T.jk[:, 256 * k:256 * k + 256], T.pre[:], F.Sign, bias=T.scl[:, 256 * k + 255:256 * k + 256],
-                                       scale=-1.0, accum_out=T.g8[:, k:k + 1]))
+        s_acc = act(T.jk[:, 256 * k:256 * k + 256], T.pre[:], F.Sign, [v_pre, v_sc[k]], bias=T.scl[:, 256 * k + 255:256 * k + 256],
+                    scale=-1.0, accum_out=T.g8[:, k:k + 1])
     v_w8 = stay(3)
-    v_ke = done("v", V.tensor_scalar(T.ke[:], T.scl[:, 255:1024:256], T.pre[:, 255:256], 512.0, A.is_ge, A.mult))
+    v_ke = ts(T.ke[:], T.scl[:, 255:1024:256], T.pre[:, 255:256], 512.0, A.is_ge, A.mult)
     need("v", d_w)
     v_wq = done("v", V.quantize_mx(T.wq[:], T.ws[:], T.wt[:]))
-    need("v", v_ke)
-    v_e = done("v", V.tensor_tensor(T.g8[:, 4:8], T.ke[:], T.scl[:, 255:1024:256], A.add))
+    v_e = tt(T.g8[:, 4:8], T.ke[:], T.scl[:, 255:1024:256], A.add, [v_ke])
 
-    need("v", s_acc, v_w8, v_e)
-    for c in range(2):
-        for h in range(2):
-            v_ab = done("v", V.tensor_tensor(T.ab[64 * h:64 * h + 64, c:16:2], T.g8[64 * c:64 * c + 64, :], T.w8[64 * c:64 * c + 64, :], A.add))
-    need("v", v_ab)
-    need("s", v_ab)
-    for q in range(2):
-        for c in range(2):
-            a, b = 32 * q, 32 * c
-            v_zb = done("v", V.tensor_copy(T.zb[a:a + 32, c:32:2], T.ab[b:b + 32, :]))
-            s_zb = done("s", S.activation(T.zb[64 + a:96 + a, c:32:2], T.ab[64 + b:96 + b, :], F.Copy))
-    need("v", v_zb, s_zb)
-    v_zt = done("v", V.transpose(T.zt[:], T.zb[:]))
-    need("v", v_zt)
-    need("s", v_zt)
+    tt(T.zz[:, 0:8], T.g8[:], T.w8[:], A.add, [s_acc, v_w8, v_e])
     for h in range(2):
-        v_bt = done("v", V.tensor_copy(T.bt[:, 16 * h:16 * h + 16], T.zt[:, 0:16]))
-        s_bt = done("s", S.activation(T.bt[:, 32 + 16 * h:48 + 16 * h], T.zt[:, 16:32], F.Copy))
-    need("v", v_bt, s_bt)
-    v_wl = done("v", V.transpose(T.wl[:], T.bt[:]))
-    need("v", v_wl)
-    for b in range(2):
-        v_fo = done("v", V.tensor_scalar(T.foff[:, b:32:2], T.wl[:, 32 * b:32 * b + 16], 0.5, 128.0, A.mult, A.add))
+        a, b = 64 * h, 64 - 64 * h
+        v_ab = tt(T.zz[a:a + 64, 8:16], T.g8[b:b + 64, :], T.w8[b:b + 64, :], A.add)
+    v_own = cp(words(T.cand[:, o:o + CAPP]), words(T.xq[:]).indirect(T.snoff[:, 2 * r:2 * r + 2]))
+    for q in range(2):
+        a, b = 32 * q, 32 * q + 32
+        v_zb = cp(T.zz[a:a + 32, 16:32], T.zz[b:b + 32, 0:16], [v_ab])
+        a, b = 64 + a, (64 + b) % 128
+        s_zb = act(T.zz[a:a + 32, 16:32], T.zz[b:b + 32, 0:16], F.Copy, [v_ab])
+    need("v", v_zb, s_zb)
+    for h in range(2):
+        v_zt = done("v", V.transpose(T.zt[:, 32 * h:32 * h + 32], T.zz[:, 0:32]))
+    need("v", v_zt)
+    v_sw = done("v", V.transpose(T.zz[:, 32:64], T.zt[:, 16:48]))
+    v_fo = ts(T.foff[:], T.zz[:].indirect(T.coff[:, 0:2]), 0.5, 128.0, A.mult, A.add, [v_sw, v_coff])
+    v_eo = ts(T.eoff[:], T.zz[:].indirect(T.coff[:, 2:3]), 256.0, None, A.add)
 
     need("v", v_fo, arrc, v_own, d_k[0], d_k[1])
     need("s", v_fo, arrs, s_own, d_k[0], d_k[1])
     v_af, s_af, t_y = [], [], []
     for k in range(2):
         a, f = 256 * k, T.foff[:, 16 * k:16 * k + 16]
-        v_af.append(done("v", V.tensor_copy(T.aft[:, a:a + 256].bitcast(dt.uint32), T.cand[:].bitcast(dt.uint32).indirect(f))))
-        s_af.append(done("s", S.activation(T.afts[:, a:a + 256], T.cands[:].indirect(f), F.Copy)))
+        v_af.append(cp(words(T.aft[:, a:a + 256]), words(T.cand[:]).indirect(f)))
+        s_af.append(act(T.afts[:, a:a + 256], T.cands[:].indirect(f), F.Copy))
         need("t", v_af[k], s_af[k], v_wq)
         t_y.append(done("t", g.tensor.matmul_mx(T["pc%d" % k][:, 0:256], T.wq[:], T.ws[:], T.aft[:, a:a + 256], T.afts[:, a:a + 256], True, True)))
         need("y", v_af[k])
         load(Y, "d_out", T.oc[:, 4 * a:4 * a + 1024], T.aft[:, a:a + 256].bitcast(dt.uint8))
     for k in range(2):
         a = 256 * k
-        need("s", t_y[k])
-        s_y = done("s", S.activation(T.ysb[:, a:a + 256], T["pc%d" % k][:, 0:256], F.Copy))
+        s_y = act(T.ysb[:, a:a + 256], T["pc%d" % k][:, 0:256], F.Copy, [t_y[k]])
         need("s" if k else "y", s_y)
         load(S if k else Y, "d_out", T.y[:, a:a + 256], T.ysb[:, a:a + 256])
-    for h in range(2):
-        for b in range(2):
-            c = 32 * b + 16 + 8 * h
-            v_eo = done("v", V.tensor_scalar(T.eoff[64 * h:64 * h + 64, b:16:2], T.wl[64 * h:64 * h + 64, c:c + 8], 256.0, None, A.add))
-    need("v", v_eo, s_ev, g_ev, v_evw)
-    a = done("v", V.tensor_copy(T.evw[:].indirect(T.eoff[:]), T.evin[:]))
-    need("v", a)
-    a = done("v", V.tensor_copy(T.evs[0:64, :], T.evw[64:128, 0:M]))
-    need("v", a)
-    v_ev = done("v", V.tensor_tensor(T.evo[0:64, :], T.evw[0:64, 0:M], T.evs[0:64, :], A.add))
+    a = cp(T.evw[:].indirect(T.eoff[:]), T.evin[:], [v_eo, s_ev, g_ev, v_evw])
+    a = cp(T.evs[0:64, :], T.evw[64:128, 0:M], [a])
+    v_ev = tt(T.evo[0:64, :], T.evw[0:64, 0:M], T.evs[0:64, :], A.add, [a])
     need("y", s_af[1])
     for k in range(4):
         d_out = load(Y, "d_out", T.osc[4 * k:4 * k + 4, :], T.afts[32 * k:32 * k + 4, :])

@@ -13,22 +13,22 @@ def _sb(n, d):
 SCRATCH = {
     "snr": _sb(16, I32), "snoff": _sb(16, U16), "vf": _sb(16, F32),
     "xt": _sb(1024, BF), "xq": _sb(256, X4), "xs": _sb(256, U8),
-    "slq": _sb(256, X4), "sls": _sb(256, U8),
-    "cand": _sb(NS + C, X4), "cands": _sb(NS + C, U8), "aft": _sb(512, X4), "afts": _sb(512, U8),
+    "slq": _sb(256, X4), "sls": _sb(256, U8), "hs": _sb(128, U8), "land": _sb(NS, X4), "lands": _sb(NS, U8),
+    "cand": _sb(2 * C, X4), "cands": _sb(2 * C, U8), "aft": _sb(512, X4), "afts": _sb(512, U8),
     "uw": _sb(4, BF), "ut": _sb(512, BF), "uq": _sb(128, X4), "us": _sb(128, U8),
     "wt": _sb(512, BF), "wq": _sb(128, X4), "ws": _sb(128, U8),
     "pi": _sb(32, I32), "p4": _sb(32, I32), "off4": _sb(32, U16), "bi": _sb(16, I32), "boff": _sb(16, U16),
-    "nn": _sb(16, I32), "nf": _sb(1, F32), "coff": _sb(4, U16),
-    "mu": _sb(128, F32), "zr": _sb(NS, BF), "j2": _sb(4, F32),
-    "lv": _sb(64, F32), "bc": _sb(256, BF), "vrow": _sb(256, BF), "pre": _sb(256, F32),
-    "sv": _sb(4, F32), "dl": _sb(4, F32), "xx": _sb(512, F32), "cm": _sb(2048, BF), "scl": _sb(1024, BF), "jk": _sb(1024, BF),
-    "ke": _sb(4, F32), "g8": _sb(8, F32), "w8": _sb(8, F32), "zz": _sb(64, F32), "zt": _sb(64, F32),
-    "foff": _sb(32, U16), "eoff": _sb(16, U16),
+    "nn": _sb(16, I32), "nf": _sb(1, F32), "coff": _sb(6, U16),
+    "mu": _sb(128, F32), "zr": _sb(NS, BF), "j2": _sb(8, F32),
+    "lv": _sb(64, I32), "bc": _sb(256, BF), "vrow": _sb(256, BF), "pre": _sb(256, F32),
+    "sv": _sb(4, F32), "dl": _sb(4, F32), "xx": _sb(512, F32), "cm": _sb(2048, BF), "scl": _sb(1280, BF), "jk": _sb(1024, BF),
+    "sg": _sb(512, BF), "acc": _sb(2, F32), "w8": _sb(8, F32), "zz": _sb(64, F32), "zt": _sb(64, F32),
+    "aoff": _sb(16, U16), "foff": _sb(32, U16), "eoff": _sb(16, U16),
     "evin": _sb(256, F32), "evw": _sb(1024, F32), "evs": _sb(128, F32), "evo": _sb(128, F32), "ysb": _sb(512, F32),
     "ra": ("psum", [128, 512], F32), "rc": ("psum", [128, 512], F32), "sa": ("psum", [128, 512], F32), "sc": ("psum", [128, 512], F32),
     "pc0": ("psum", [128, 512], F32), "pc1": ("psum", [128, 512], F32), "pc2": ("psum", [128, 512], F32), "pc3": ("psum", [128, 512], F32),
 }
-SEMAPHORES = ["v", "s", "t", "gq", "d_sn", "d_x", "d_u", "d_k0", "d_k1", "d_w", "d_ev", "d_out", "larr", "arrc", "arrs", "loc"]
+SEMAPHORES = ["v", "s", "t", "gq", "d_sn", "d_x", "d_u", "d_k0", "d_k1", "d_w", "d_ev", "d_out", "larr", "arrc", "arrs", "harr", "loc"]
 
 
 def _deal(dst, engs):
@@ -48,17 +48,54 @@ def _engines(T, topo, s):
     off = [d for d in rest if topo.chip(T.cores[d]) != topo.chip(me)]
     e_off = topo.engines(me, T.cores[off[0]])
     e_on = [e for e in topo.engines(me, T.cores[on[0]]) if e not in e_off]
-    h = len(e_off) // 2
-    a = _deal(off, e_off)
-    b = _deal(off[2:] + off[:2], e_off[h:] + e_off[:h])
-    a[on[0]] = b[on[0]] = e_on[:len(e_on) // 4]
-    return a, b
+    a = _deal(off, e_off[0::2] + e_off[1::2])
+    b = _deal(off[2:] + off[:2], e_off[1::2] + e_off[0::2])
+    a[on[0]] = b[on[0]] = e_on[:2]
+    return b, a, e_on
+
+
+def _helpers(T, topo, s):
+    me = T.cores[s]
+    idle = [c for c in topo.cores_of(me) if c not in T.cores]
+    k = [c for c in topo.cores_of(me) if c in T.cores].index(me)
+    near = [c for c in idle if topo.die(c) == topo.die(me)][k]
+    far = [c for c in idle if all(topo.may_write(c, d) for d in T.cores)][k]
+    mine = [d for d in range(N) if topo.may_write(near, T.cores[d])]
+    return [(near, mine), (far, [d for d in range(N) if d not in mine])]
+
+
+def _hand_on(topo, T, s, h):
+    core, dst = _helpers(T, topo, s)[h]
+    off = [d for d in dst if topo.chip(T.cores[d]) != topo.chip(core)]
+    e_off = topo.engines(core, T.cores[off[0]])
+    w = len(e_off) // len(off)
+    r = {d: e_off[w * k:w * k + w] for k, d in enumerate(off)}
+    for d in dst:
+        if d not in off and d != s:
+            r[d] = [e for e in topo.engines(core, T.cores[d]) if e not in e_off][:2]
+    return r
+
+
+def _transfer(topo, core, engs, src, dst, sem):
+    rid, pid, _ = topo.addr(core)
+    return RemoteDMATransfer(dst_ids=[DstId(rid=rid, pnc=pid)], dma_engine_mask=sum(1 << e for e in engs), remote_sem=sem, srcs=[src], dsts=[dst])
+
+
+def helper_program(g, core, T, topo):
+    for s in range(N):
+        for h, (c, dst) in enumerate(_helpers(T, topo, s)):
+            if c == core:
+                engs = _hand_on(topo, T, s, h)
+                g.wait_ge(T.sem.harr, 4)
+                g.remote_dma_fused([_transfer(topo, T.cores[d], e, T.hs[:, CAPP * dst.index(d):CAPP * dst.index(d) + CAPP],
+                                              T.lands[:, CAPP * s:CAPP * s + CAPP], T.sem.arrs) for d, e in engs.items()], local_sem=T.sem.loc)
+                g.wait_ge(T.sem.loc, sum(len(e) for e in engs.values()))
 
 
 def rank_program(g, core, T, topo):
     r = T.rank_of(core)
     if r is None:
-        return
+        return helper_program(g, core, T, topo)
     sem = T.sem
     cnt = {"v": 0, "s": 0, "t": 0, "gq": 0}
     seen = {}
@@ -112,42 +149,40 @@ def rank_program(g, core, T, topo):
     d_k = []
     for k in range(2):
         a, b = 256 * k, 256 * k + 256
-        load(Y, "d_k%d" % k, T.cand[:, NS + a:NS + b].bitcast(dt.uint8), T.kc[:, 4 * a:4 * b])
-        d_k.append(load(Y, "d_k%d" % k, T.cands[:, NS + a:NS + b], T.ks[:, a:b]))
+        load(Y, "d_k%d" % k, T.cand[:, C + a:C + b].bitcast(dt.uint8), T.kc[:, 4 * a:4 * b])
+        d_k.append(load(Y, "d_k%d" % k, T.cands[:, C + a:C + b], T.ks[:, a:b]))
     d_w = load(Y, "d_w", T.wt[:], T.w[:])
 
     SH, AND = A.arith_shift_right, A.bitwise_and
     g_pi = done("gq", g.iota(T.pi[:], [[128, 8], [0, 4]], 0, 1))
     v_mu = done("v", V.memset(T.mu[:], 1.0))
-    v_zr = done("v", V.memset(T.zr[:], 0.0))
-    v_ev0 = done("v", V.memset(T.evw[:, 0:M], 0.0))
+    done("v", V.memset(T.scl[:, 1278:1280], -512.0))
+    done("v", V.memset(T.zz[:, 0:16], 0.0))
     need("gq", v_mu)
     g_mu = done("gq", g.affine_select(T.mu[:], T.mu[:], [[-1, 128]], A.is_gt, 0.0, 0, 1))
-    g_j2 = done("gq", g.iota(T.j2[:], [[256, 4]], 0, 2, allow_small_or_imprecise_dtypes=True))
     p, nn = T.pi[:, 0:1], lambda k: T.nn[:, k:k + 1]
     a4 = ts(T.p4[:], T.pi[:], 3, None, AND, deps=[g_pi])
-    ab = ts(T.bi[:], T.pi[:, 0:32:2], 4, 0x79, SH, AND)
     n1 = ts(nn(0), p, 0x66, None, AND)
-    v_off4 = cp(T.off4[:], T.p4[:], [a4])
-    v_boff = cp(T.boff[:], T.bi[:], [ab])
-    n2 = ts(nn(1), nn(0), 15, 31, A.mult, A.add, [n1])
+    ab = ts(T.bi[:], T.pi[:, 0:32:2], 4, 0x79, SH, AND)
     n5 = ts(nn(2), p, 34, None, A.mult)
-
-    v_vf = ts(T.vf[:], T.snr[:], 0.0, None, A.is_ge, deps=[d_sn])
-    v_sno = cp(T.snoff[:], T.snr[:])
-    v_lv = ts(T.lv[:, 8 * r:8 * r + 2], T.snr[:, 2 * r:2 * r + 2], 0.0, None, A.is_ge)
-
+    v_off4 = cp(T.off4[:], T.p4[:], [a4])
+    n2 = ts(nn(1), nn(0), 15, 31, A.mult, A.add, [n1])
+    v_boff = cp(T.boff[:], T.bi[:], [ab])
+    ts(nn(5), nn(2), 32, None, AND, deps=[n5])
     ts(nn(3), nn(1), 1, 16, SH, AND, [n2])
     ts(nn(4), nn(1), 3, 8, SH, AND)
-    ts(nn(5), nn(2), 32, None, AND, deps=[n5])
     a = ts(nn(6), p, 3, 1, SH, AND)
-    ts(T.nn[:, 8:10], T.pi[:, 0:8:4], 6, 2, SH, AND)
-    ts(nn(10), T.pi[:, 4:5], 5, 6, SH, AND)
-    done("v", V.memset(T.w8[:, 4:8], 0.0))
-    a = tt(T.nn[:, 12:14], T.nn[:, 3:5], T.nn[:, 5:7], A.add, [a])
-    need("v", v_ev0)
-    v_evw = done("v", V.memset(T.evw[0:32, 0:M], -1.0))
-    v_nf = tt(T.nf[:], nn(12), nn(13), A.add, [a])
+    ts(T.nn[:, 8:12], T.pi[:, 0:16:4], 6, 6, SH, AND)
+    ts(nn(12), p, 5, 2, SH, AND)
+    a = tt(T.nn[:, 13:15], T.nn[:, 3:5], T.nn[:, 5:7], A.add, [a])
+    helpers = _helpers(T, topo, r)
+    order = helpers[0][1] + helpers[1][1]
+    at = {d: k for k, d in enumerate(order)}
+    for k in range(0, N, 2):
+        v_sno = cp(T.snoff[:, 2 * k:2 * k + 4], T.snr[:, 2 * order[k]:2 * order[k] + 4], [d_sn])
+    v_lv = cp(T.lv[:, 8 * r:8 * r + 2], T.snr[:, 2 * r:2 * r + 2])
+    v_nf = tt(T.nf[:], nn(13), nn(14), A.add, [a])
+    v_coff = ts(T.coff[:, 0:5], T.nn[:, 8:13], T.nf[:], None, A.add, deps=[v_nf])
 
     s_ut = act(T.ut[:], T.uw[:].indirect(T.off4[:]), F.Copy, [v_off4, d_u])
 
@@ -156,78 +191,74 @@ def rank_program(g, core, T, topo):
     need("v", s_ut)
     v_uq = done("v", V.quantize_mx(T.uq[:], T.us[:], T.ut[:]))
     v_sl = cp(words(T.slq[:]), words(T.xq[:]).indirect(T.snoff[:, 0:16]), [v_xq, v_sno])
-    v_coff = ts(T.coff[:, 0:3], T.nn[:, 8:11], T.nf[:], None, A.add, deps=[v_nf])
     s_sl = act(T.sls[:], T.xs[:].indirect(T.snoff[:, 0:16]), F.Copy, [v_xq, v_sno])
     o = CAPP * r
 
-    local = [0]
-
-    def send(engs, src, dst, rs):
-        tr = []
-        for d, es in engs.items():
-            rid, pid, _ = topo.addr(T.cores[d])
-            m = 0
-            for e in es:
-                m |= 1 << e
-            tr.append(RemoteDMATransfer(dst_ids=[DstId(rid=rid, pnc=pid)], dma_engine_mask=m, remote_sem=sem[rs],
-                                        srcs=[src(d)], dsts=[dst]))
-            local[0] += len(es)
-        g.remote_dma_fused(tr, local_sem=sem["loc"])
-
-    ec, es = _engines(T, topo, r)
-    need("gq", v_vf)
-    send(ec, lambda d: T.vf[:, 2 * d:2 * d + 2], T.lv[:, 8 * r:8 * r + 2], "larr")
-    need("gq", v_sl)
-    send(ec, lambda d: T.slq[:, CAPP * d:CAPP * d + CAPP].bitcast(dt.uint8), T.cand[:, o:o + CAPP].bitcast(dt.uint8), "arrc")
+    el, ec, eh = _engines(T, topo, r)
+    need("gq", d_sn)
+    tr = [_transfer(topo, T.cores[d], e, T.snr[:, 2 * d:2 * d + 2], T.lv[:, 8 * r:8 * r + 2], sem.larr) for d, e in el.items()]
+    g.remote_dma_fused(tr, local_sem=sem.loc)
+    g_j2 = done("gq", g.iota(T.j2[:], [[128, 8]], 0, 1, allow_small_or_imprecise_dtypes=True))
     need("gq", s_sl)
-    send(es, lambda d: T.sls[:, CAPP * d:CAPP * d + CAPP], T.cands[:, o:o + CAPP], "arrs")
-    nc = sum(len(_engines(T, topo, s)[0][r]) for s in range(N) if s != r)
-    nl = sum(len(_engines(T, topo, s)[1][r]) for s in range(N) if s != r)
-    larr, arrc, arrs = ("larr", nc), ("arrc", nc), ("arrs", nl)
-    need("gq", g_j2)
+    tr = [_transfer(topo, c, eh[4 * h:4 * h + 4], T.sls[:, 128 * h:128 * h + 128], T.hs[:], sem.harr) for h, (c, _) in enumerate(helpers)]
+    g.remote_dma_fused(tr, local_sem=sem.loc)
+    need("gq", v_sl)
+    tr = [_transfer(topo, T.cores[d], e, T.slq[:, CAPP * at[d]:CAPP * at[d] + CAPP].bitcast(dt.uint8), T.land[:, o:o + CAPP].bitcast(dt.uint8), sem.arrc)
+          for d, e in ec.items()]
+    g.remote_dma_fused(tr, local_sem=sem.loc)
+    local = sum(len(e) for e in el.values()) + sum(len(e) for e in ec.values()) + len(eh)
+    larr, arrc = [(nm, sum(len(_engines(T, topo, s)[i][r]) for s in range(N) if s != r)) for i, nm in enumerate(("larr", "arrc"))]
+    arrs = ("arrs", sum(len(_hand_on(topo, T, s, h).get(r, [])) for s in range(N) for h in range(2)))
+    v_zr = done("gq", g.iota(T.zr[:], [[0, NS]], 0, 0, allow_small_or_imprecise_dtypes=True))
     g_ev = done("gq", g.iota(T.evin[0:32, :], [[1, 256]], 0, 0, allow_small_or_imprecise_dtypes=True))
     need("gq", g_ev)
     g_ev = done("gq", g.iota(T.evin[64:96, :], [[1, 256]], 257, 0, allow_small_or_imprecise_dtypes=True))
 
     need("t", v_uq)
-    t_pc, t_r, t_s = [], [], []
+    t_pc, t_r, t_s = {}, {}, {}
 
     def row(nm, h):
-        a = NS + 256 * h
+        a = C + 256 * h
         return done("t", g.tensor.matmul_mx(T[nm + "ac"[h]][:, 0:256], T.uq[:], T.us[:], T.cand[:, a:a + 256],
                                             T.cands[:, a:a + 256], True, True))
 
-    for h in range(2):
-        need("t", d_k[h])
-        for k in (2 * h, 2 * h + 1):
-            a = NS + 128 * k
-            t_pc.append(done("t", g.tensor.matmul_mx(T["pc%d" % k][:, 0:128], T.cand[:, a:a + 128], T.cands[:, a:a + 128],
-                                                     T.uq[:], T.us[:], True, True)))
-        t_r.append(row("r", h))
-    for h in range(2):
-        t_s.append(row("s", h))
+    def col(k):
+        a = C + 128 * k
+        t_pc[k] = done("t", g.tensor.matmul_mx(T["pc%d" % k][:, 0:128], T.cand[:, a:a + 128], T.cands[:, a:a + 128], T.uq[:], T.us[:], True, True))
 
-    v_sv = {}
+    need("t", d_k[0])
+    col(1)
+    col(0)
+    t_r[0] = row("r", 0)
+    need("t", d_k[1])
+    t_r[1] = row("r", 1)
+    col(2)
+    col(3)
+    for h in (1, 0):
+        t_s[h] = row("s", h)
+
+    v_sv, s_x, s_dl, s_acc, s_ev, v_cm, v_sc = {}, {}, {}, {}, {}, {}, {}
     for k in (1, 0):
         v_sv[k] = cp(T.sv[:, k:k + 1], T["pc%d" % k][:, 0:1], [t_pc[k]])
-    s_x = {}
 
-    def thresholds(h):
-        a = act(T.dl[:, 2 * h:2 * h + 2], T.sv[:, 2 * h:2 * h + 2], F.Abs, [v_sv[2 * h], v_sv[2 * h + 1], g_mu],
-                scale=0.74 * 2.0 ** -23, bias=2e-38)
-        for k in (2 * h, 2 * h + 1):
-            s_x[k] = act(T.xx[:, 128 * k:128 * k + 128], T.mu[:], F.Identity, [a], bias=T.sv[:, k:k + 1], scale=T.dl[:, k:k + 1])
+    def step(h):
+        s_dl[h] = act(T.dl[:, 2 * h:2 * h + 2], T.sv[:, 2 * h:2 * h + 2], F.Abs, [v_sv[2 * h], v_sv[2 * h + 1], g_mu],
+                      scale=0.74 * 2.0 ** -23, bias=2e-38)
 
-    thresholds(0)
-    for k in range(2, 4):
+    def threshold(k):
+        s_x[k] = act(T.xx[:, 128 * k:128 * k + 128], T.mu[:], F.Identity, [s_dl[k // 2]], bias=T.sv[:, k:k + 1], scale=T.dl[:, k:k + 1])
+
+    def signs(k):
+        s_acc[k] = act(T.sg[:, 256 * k:256 * k + 256], T.sc[:, 0:256], F.Sign, [t_s[1], v_sv[k]], bias=T.sv[:, k:k + 1], scale=-1.0)
+
+    def below(k):
+        s_acc[k] = act(T.jk[:, 256 * k:256 * k + 256], T.sg[:, 256 * k:256 * k + 256], F.Relu, [s_acc[k]], accum_out=T.acc[:, k:k + 1])
+
+    def column(k):
         v_sv[k] = act(T.sv[:, k:k + 1], T["pc%d" % k][:, 0:1], F.Copy, [t_pc[k]])
-    s_bc = act(T.bc[:], T.lv[:].indirect(T.boff[:]), F.Copy, [larr, v_lv, v_boff])
-    thresholds(1)
-    s_own = act(T.cands[:, o:o + CAPP], T.xs[:].indirect(T.snoff[:, 2 * r:2 * r + 2]), F.Copy)
-    for h in range(2):
-        s_ev = act(T.evin[32 + 64 * h:64 + 64 * h, :], T["s" + "ac"[h]][32 + 64 * h:64 + 64 * h, 0:256], F.Copy, [t_s[h]])
 
-    v_cm, v_sc = {}, {}
+    def scores(h):
+        s_ev[h] = act(T.evin[32 + 64 * h:64 + 64 * h, :], T["s" + "ac"[h]][32 + 64 * h:64 + 64 * h, 0:256], F.Copy, [t_s[h]])
 
     def outer(k, h, lo, hi, op):
         v_cm[k] = ts(T.cm[:, 512 * k + 256 * h + lo:512 * k + 256 * h + hi], T["r" + "ac"[h]][:, lo:hi],
@@ -239,66 +270,78 @@ def rank_program(g, core, T, topo):
                      [s_x[k], t_r[k // 2]])
 
     def total(k):
-        need("v", v_cm[k])
-        v_sc[k] = done("v", V.tensor_tensor_scan(T.scl[:, 256 * k:256 * k + 256], T.cm[:, 512 * k:512 * k + 256],
-                                                 T.cm[:, 512 * k + 256:512 * k + 512], -256.0, A.add, A.add))
+        n, first = (128, T.acc[:, k:k + 1]) if k in s_acc else (256, 0.0)
+        need("v", v_cm[k], *([s_acc[k]] if k in s_acc else []))
+        v_sc[k] = done("v", V.tensor_tensor_scan(T.scl[:, 256 * k + 256 - n:256 * k + 256], T.cm[:, 512 * k:512 * k + n],
+                                                 T.cm[:, 512 * k + n:512 * k + 2 * n], first, A.add, A.add))
 
     def stay(k):
-        return ts(T.w8[:, k:k + 1], T.scl[:, 256 * k + 255:256 * k + 256], T.pre[:, 255:256], T.j2[:, k:k + 1], A.is_ge, A.mult,
+        return ts(T.w8[:, k:k + 1], T.scl[:, 256 * k + 255:256 * k + 256], T.pre[:, 255:256], T.j2[:, 4 + k:5 + k], A.is_ge, A.mult,
                   [v_sc[k], v_pre, g_j2])
 
+    step(0)
     outer(1, 0, 0, 128, A.is_le)
     outer(0, 0, 128, 256, A.is_lt)
+    column(2)
+    column(3)
+    threshold(0)
+    step(1)
+    for k in (1, 2, 3):
+        threshold(k)
+    s_bc = act(T.bc[:], T.lv[:].indirect(T.boff[:]), F.Sign, [larr, v_lv, v_boff], bias=1.0)
+    signs(1)
+    below(1)
+    scores(0)
     outer(0, 1, 0, 256, A.is_lt)
-    outer(1, 1, 0, 256, A.is_lt)
-    inner(0)
-    inner(1)
+    outer(2, 1, 128, 256, A.is_lt)
     outer(2, 0, 0, 256, A.is_le)
-    total(0)
+    inner(0)
     outer(3, 0, 0, 256, A.is_le)
+    for k in (2, 3, 1):
+        inner(k)
+    total(0)
     need("v", s_bc)
     v_vr = done("v", V.transpose(T.vrow[:], T.bc[:]))
-    total(1)
-    need("v", v_vr, v_zr)
-    v_pre = done("v", V.tensor_tensor_scan(T.pre[:], T.vrow[:], T.zr[:], -256.5, A.add, A.add))
-    outer(2, 1, 128, 256, A.is_lt)
-    inner(2)
-    stay(0)
     outer(3, 1, 0, 128, A.is_le)
     total(2)
-    inner(3)
-    stay(1)
+    need("v", v_vr, v_zr)
+    v_pre = done("v", V.tensor_tensor_scan(T.pre[:], T.vrow[:], T.zr[:], -0.5, A.add, A.add))
+    s_a = act(T.jk[:, 512:767], T.pre[:, 0:255], F.Sign, [v_pre, g_j2], bias=T.j2[:, 0:1], scale=-1.0, accum_out=T.w8[:, 4:5])
+    s_own = act(T.lands[:, o:o + CAPP], T.xs[:].indirect(T.snoff[:, 2 * at[r]:2 * at[r] + 2]), F.Copy)
     total(3)
-    stay(2)
-    for k in range(4):
-        s_acc = act(T.jk[:, 256 * k:256 * k + 256], T.pre[:], F.Sign, [v_pre, v_sc[k]], bias=T.scl[:, 256 * k + 255:256 * k + 256],
-                    scale=-1.0, accum_out=T.g8[:, k:k + 1])
-    v_w8 = stay(3)
-    v_ke = ts(T.ke[:], T.scl[:, 255:1024:256], T.pre[:, 255:256], 512.0, A.is_ge, A.mult)
-    need("v", d_w)
-    v_wq = done("v", V.quantize_mx(T.wq[:], T.ws[:], T.wt[:]))
-    v_e = tt(T.g8[:, 4:8], T.ke[:], T.scl[:, 255:1024:256], A.add, [v_ke])
+    total(1)
+    for k in (0, 2, 3, 1):
+        v_w8 = stay(k)
 
-    tt(T.zz[:, 0:8], T.g8[:], T.w8[:], A.add, [s_acc, v_w8, v_e])
+    tt(T.zz[:, 0:5], T.scl[:, 255:1280:256], T.w8[:, 0:5], A.max, [s_a, v_w8])
     for h in range(2):
         a, b = 64 * h, 64 - 64 * h
-        v_ab = tt(T.zz[a:a + 64, 8:16], T.g8[b:b + 64, :], T.w8[b:b + 64, :], A.add)
-    v_own = cp(words(T.cand[:, o:o + CAPP]), words(T.xq[:]).indirect(T.snoff[:, 2 * r:2 * r + 2]))
+        v_ab = tt(T.zz[a:a + 64, 8:13], T.scl[b:b + 64, 255:1280:256], T.w8[b:b + 64, 0:5], A.max)
+    v_own = cp(words(T.land[:, o:o + CAPP]), words(T.xq[:]).indirect(T.snoff[:, 2 * at[r]:2 * at[r] + 2]))
     for q in range(2):
         a, b = 32 * q, 32 * q + 32
         v_zb = cp(T.zz[a:a + 32, 16:32], T.zz[b:b + 32, 0:16], [v_ab])
         a, b = 64 + a, (64 + b) % 128
         s_zb = act(T.zz[a:a + 32, 16:32], T.zz[b:b + 32, 0:16], F.Copy, [v_ab])
+    scores(1)
+    need("v", d_w)
+    v_wq = done("v", V.quantize_mx(T.wq[:], T.ws[:], T.wt[:]))
     need("v", v_zb, s_zb)
     for h in range(2):
         v_zt = done("v", V.transpose(T.zt[:, 32 * h:32 * h + 32], T.zz[:, 0:32]))
+    done("v", V.memset(T.evw[:, 0:M], 0.0))
     need("v", v_zt)
     v_sw = done("v", V.transpose(T.zz[:, 32:64], T.zt[:, 16:48]))
-    v_fo = ts(T.foff[:], T.zz[:].indirect(T.coff[:, 0:2]), 0.5, 128.0, A.mult, A.add, [v_sw, v_coff])
-    v_eo = ts(T.eoff[:], T.zz[:].indirect(T.coff[:, 2:3]), 256.0, None, A.add)
+    need("v", (v_sw[0], v_sw[1] - 1))
+    v_evw = done("v", V.memset(T.evw[0:32, 0:M], -1.0))
+    v_ao = ts(T.aoff[:], T.zz[:].indirect(T.coff[:, 2:3]), 0.5, 127.5, A.mult, A.add, [v_sw, v_coff])
+    v_fo = cp(T.foff[:], T.zz[:].indirect(T.coff[:, 0:2]))
+    v_eo = cp(T.eoff[:], T.zz[:].indirect(T.coff[:, 4:5]))
+    v_arr = cp(words(T.cand[:, 0:M]), words(T.land[:]).indirect(T.aoff[:, 0:8]), [v_ao, arrc, v_own])
+    s_arr = act(T.cands[:, 0:M], T.lands[:].indirect(T.aoff[:, 0:8]), F.Copy, [v_ao, arrs, s_own])
 
-    need("v", v_fo, arrc, v_own, d_k[0], d_k[1])
-    need("s", v_fo, arrs, s_own, d_k[0], d_k[1])
+    need("v", v_fo, v_arr, d_k[0], d_k[1])
+    need("s", v_fo, s_arr, d_k[0], d_k[1])
     v_af, s_af, t_y = [], [], []
     for k in range(2):
         a, f = 256 * k, T.foff[:, 16 * k:16 * k + 16]
@@ -313,9 +356,8 @@ def rank_program(g, core, T, topo):
         s_y = act(T.ysb[:, a:a + 256], T["pc%d" % k][:, 0:256], F.Copy, [t_y[k]])
         need("s" if k else "y", s_y)
         load(S if k else Y, "d_out", T.y[:, a:a + 256], T.ysb[:, a:a + 256])
-    a = cp(T.evw[:].indirect(T.eoff[:]), T.evin[:], [v_eo, s_ev, g_ev, v_evw])
-    a = cp(T.evs[0:64, :], T.evw[64:128, 0:M], [a])
-    v_ev = tt(T.evo[0:64, :], T.evw[0:64, 0:M], T.evs[0:64, :], A.add, [a])
+    a = cp(T.evw[:].indirect(T.eoff[:]), T.evin[:], [v_eo, s_ev[1], g_ev, v_evw])
+    v_ev = tt(T.evo[0:64, :], T.evw[0:64, 0:M], T.evw[64:128, 0:M], A.add, [a])
     need("y", s_af[1])
     for k in range(4):
         d_out = load(Y, "d_out", T.osc[4 * k:4 * k + 4, :], T.afts[32 * k:32 * k + 4, :])
@@ -327,4 +369,4 @@ def rank_program(g, core, T, topo):
     for n, val in cnt.items():
         need("y", (n, val))
     need("y", d_ev, d_out)
-    need("gq", ("loc", local[0]))
+    need("gq", ("loc", local))

@@ -11,34 +11,28 @@ def _sb(n, d):
 
 
 SCRATCH = {
-    "snr": _sb(16, I32), "snoff": _sb(16, U16), "vf": _sb(16, F32),
+    "lv": _sb(256, I32), "snoff": _sb(16, U16),
     "xt": _sb(1024, BF), "xq": _sb(256, X4), "xs": _sb(256, U8),
-    "slq": _sb(256, X4), "sls": _sb(256, U8), "hs": _sb(128, U8), "land": _sb(NS, X4), "lands": _sb(NS, U8),
+    "slq": _sb(256, X4), "sls": _sb(256, U8), "hs": _sb(128, U8), "hq": _sb(64, X4), "land": _sb(NS, X4), "lands": _sb(NS, U8),
     "cand": _sb(2 * C, X4), "cands": _sb(2 * C, U8), "aft": _sb(512, X4), "afts": _sb(512, U8),
-    "uw": _sb(4, BF), "ut": _sb(512, BF), "uq": _sb(128, X4), "us": _sb(128, U8),
+    "ut": _sb(520, BF), "uq": _sb(130, X4), "us": _sb(130, U8), "uoff": _sb(8, U16), "rq": _sb(128, X4), "rs": _sb(128, U8),
     "wt": _sb(512, BF), "wq": _sb(128, X4), "ws": _sb(128, U8),
-    "pi": _sb(32, I32), "p4": _sb(32, I32), "off4": _sb(32, U16), "bi": _sb(16, I32), "boff": _sb(16, U16),
-    "nn": _sb(16, I32), "nf": _sb(1, F32), "coff": _sb(6, U16),
-    "mu": _sb(128, F32), "zr": _sb(NS, BF), "j2": _sb(8, F32),
-    "lv": _sb(64, I32), "bc": _sb(256, BF), "vrow": _sb(256, BF), "pre": _sb(256, F32),
-    "sv": _sb(4, F32), "dl": _sb(4, F32), "xx": _sb(512, F32), "cm": _sb(2048, BF), "scl": _sb(1280, BF), "jk": _sb(1024, BF),
-    "sg": _sb(512, BF), "acc": _sb(2, F32), "w8": _sb(8, F32), "zz": _sb(64, F32), "zt": _sb(64, F32),
-    "aoff": _sb(16, U16), "foff": _sb(32, U16), "eoff": _sb(16, U16),
-    "evin": _sb(256, F32), "evw": _sb(1024, F32), "evs": _sb(128, F32), "evo": _sb(128, F32), "ysb": _sb(512, F32),
-    "ra": ("psum", [128, 512], F32), "rc": ("psum", [128, 512], F32), "sa": ("psum", [128, 512], F32), "sc": ("psum", [128, 512], F32),
-    "pc0": ("psum", [128, 512], F32), "pc1": ("psum", [128, 512], F32), "pc2": ("psum", [128, 512], F32), "pc3": ("psum", [128, 512], F32),
+    "pi": _sb(16, I32), "bi": _sb(16, I32), "boff": _sb(16, U16), "nn": _sb(16, I32), "coff": _sb(6, U16),
+    "mu": _sb(128, F32), "j2": _sb(16, F32), "kk": _sb(4, F32),
+    "bc": _sb(256, BF), "vrow": _sb(256, BF), "pre": _sb(258, BF),
+    "sv": _sb(4, F32), "dl": _sb(4, F32), "xx": _sb(512, F32), "cm": _sb(2048, BF), "scl": _sb(2048, BF), "jk": _sb(1024, BF),
+    "sg": _sb(512, BF), "acc": _sb(2, F32), "a2": _sb(136, F32), "zz": _sb(32, F32), "zt": _sb(96, F32), "zu": _sb(128, F32),
+    "aoff": _sb(16, U16), "foff": _sb(48, U16),
+    "evin": _sb(256, F32), "evw": _sb(1024, F32), "evo": _sb(128, F32), "ysb": _sb(512, F32),
 }
-SEMAPHORES = ["v", "s", "t", "gq", "d_sn", "d_x", "d_u", "d_k0", "d_k1", "d_w", "d_ev", "d_out", "larr", "arrc", "arrs", "harr", "loc"]
+for _n in ("r0", "r1", "s0", "s1", "cv0", "cv1"):
+    SCRATCH[_n] = ("psum", [128, 512], F32)
+SEMAPHORES = ["v", "s", "t", "gq", "d_sn", "d_x", "d_u", "d_k0", "d_k1", "d_w", "d_ev", "d_out", "larr", "arrc", "arrs", "harr", "harq", "loc"]
 
 
-def _deal(dst, engs):
-    r, k = {}, 0
-    two = len(engs) - len(dst)
-    for n, d in enumerate(dst):
-        w = 2 if n >= len(dst) - two else 1
-        r[d] = engs[k:k + w]
-        k += w
-    return r
+def _share(dst, engs):
+    w = len(engs) // len(dst)
+    return {d: engs[w * k:w * k + w] for k, d in enumerate(dst)}
 
 
 def _engines(T, topo, s):
@@ -48,28 +42,28 @@ def _engines(T, topo, s):
     off = [d for d in rest if topo.chip(T.cores[d]) != topo.chip(me)]
     e_off = topo.engines(me, T.cores[off[0]])
     e_on = [e for e in topo.engines(me, T.cores[on[0]]) if e not in e_off]
-    a = _deal(off, e_off[0::2] + e_off[1::2])
-    b = _deal(off[2:] + off[:2], e_off[1::2] + e_off[0::2])
-    a[on[0]] = b[on[0]] = e_on[:2]
-    return b, a, e_on
+    (_, mine), (_, others) = _helpers(T, topo, s)
+    lists = [{**_share(off[:4], e_off[0::2]), **_share(off[4:], e_off[1::2])}]
+    codes = {**_share(off[2:], e_off[1::2]), **_share(off[:2], e_off[0::2])}
+    lists[0][on[0]], codes[on[0]] = e_on[:2], e_on[:4]
+    return lists, codes, [e_on[:4], e_on[4:]], {}
 
 
 def _helpers(T, topo, s):
     me = T.cores[s]
-    idle = [c for c in topo.cores_of(me) if c not in T.cores]
+    idle = [c for c in topo.cores_of(me) if c not in T.cores and topo.die(c) != topo.die(me)]
     k = [c for c in topo.cores_of(me) if c in T.cores].index(me)
-    near = [c for c in idle if topo.die(c) == topo.die(me)][k]
-    far = [c for c in idle if all(topo.may_write(c, d) for d in T.cores)][k]
-    mine = [d for d in range(N) if topo.may_write(near, T.cores[d])]
-    return [(near, mine), (far, [d for d in range(N) if d not in mine])]
+    far = [c for c in idle if all(topo.may_write(c, d) for d in T.cores)]
+    mid = [c for c in idle if c not in far][k]
+    mine = [d for d in range(N) if topo.may_write(mid, T.cores[d])]
+    return [(mid, mine), (far[k], [d for d in range(N) if d not in mine])]
 
 
 def _hand_on(topo, T, s, h):
     core, dst = _helpers(T, topo, s)[h]
     off = [d for d in dst if topo.chip(T.cores[d]) != topo.chip(core)]
     e_off = topo.engines(core, T.cores[off[0]])
-    w = len(e_off) // len(off)
-    r = {d: e_off[w * k:w * k + w] for k, d in enumerate(off)}
+    r = _share(off, e_off)
     for d in dst:
         if d not in off and d != s:
             r[d] = [e for e in topo.engines(core, T.cores[d]) if e not in e_off][:2]
@@ -86,10 +80,18 @@ def helper_program(g, core, T, topo):
         for h, (c, dst) in enumerate(_helpers(T, topo, s)):
             if c == core:
                 engs = _hand_on(topo, T, s, h)
-                g.wait_ge(T.sem.harr, 4)
+                g.wait_ge(T.sem.harr, len(_engines(T, topo, s)[2][h]))
                 g.remote_dma_fused([_transfer(topo, T.cores[d], e, T.hs[:, CAPP * dst.index(d):CAPP * dst.index(d) + CAPP],
                                               T.lands[:, CAPP * s:CAPP * s + CAPP], T.sem.arrs) for d, e in engs.items()], local_sem=T.sem.loc)
-                g.wait_ge(T.sem.loc, sum(len(e) for e in engs.values()))
+                local = sum(len(e) for e in engs.values())
+                if h == 0 and _engines(T, topo, s)[3]:
+                    far = _engines(T, topo, s)[3]
+                    g.wait_ge(T.sem.harq, sum(len(e) for e in far.values()))
+                    g.remote_dma_fused([_transfer(topo, T.cores[d], engs[d], T.hq[:, CAPP * k:CAPP * k + CAPP].bitcast(dt.uint8),
+                                                  T.land[:, CAPP * s:CAPP * s + CAPP].bitcast(dt.uint8), T.sem.arrc) for k, d in enumerate(far)],
+                                       local_sem=T.sem.loc)
+                    local += sum(len(engs[d]) for d in far)
+                g.wait_ge(T.sem.loc, local)
 
 
 def rank_program(g, core, T, topo):
@@ -134,17 +136,25 @@ def rank_program(g, core, T, topo):
         need("v", *deps)
         return done("v", V.tensor_copy(out, in_))
 
+    def turn(out, in_, deps=()):
+        need("v", *deps)
+        return done("v", V.transpose(out, in_))
+
     def act(out, in_, func, deps=(), **kw):
         need("s", *deps)
         return done("s", S.activation(out, in_, func, **kw))
 
+    def fill(out, pattern, base, step):
+        return done("gq", g.iota(out, pattern, base, step, allow_small_or_imprecise_dtypes=True))
+
     def words(ap):
         return ap.bitcast(dt.uint32)
 
+    l0 = 30 * r
     for k in range(4):
-        load(Y, "d_sn", T.snr[16 * k:16 * k + 16, :], T.sn[:])
-        d_sn = load(S, "d_sn", T.snr[64 + 16 * k:80 + 16 * k, :], T.sn[:])
-    d_u = load(S, "d_u", T.uw[:], T.u[:, 0:4])
+        load(Y, "d_sn", T.lv[16 * k:16 * k + 16, l0:l0 + 16], T.sn[:])
+        d_sn = load(S, "d_sn", T.lv[64 + 16 * k:80 + 16 * k, l0:l0 + 16], T.sn[:])
+    d_u = load(S, "d_u", T.ut[:, 8:16], T.u[:, 0:8])
     d_x = load(Y, "d_x", T.xt[:], T.x[:])
     d_k = []
     for k in range(2):
@@ -154,213 +164,217 @@ def rank_program(g, core, T, topo):
     d_w = load(Y, "d_w", T.wt[:], T.w[:])
 
     SH, AND = A.arith_shift_right, A.bitwise_and
-    g_pi = done("gq", g.iota(T.pi[:], [[128, 8], [0, 4]], 0, 1))
+    nn = lambda k: T.nn[:, k:k + 1]
+    done("gq", g.iota(T.pi[:], [[512, 8], [0, 2]], 0, 1))
+    done("gq", g.iota(nn(0), [[0, 1]], 15, 15))
+    g_pi = done("gq", g.iota(nn(1), [[0, 1]], 0, 68))
+    fill(T.j2[:, 0:1], [[0, 1]], 0, 1)
+    g_j2 = fill(T.j2[:, 8:16], [[256, 2], [-128, 2], [4096, 2]], C + 128 - 4096, 1)
     v_mu = done("v", V.memset(T.mu[:], 1.0))
-    done("v", V.memset(T.scl[:, 1278:1280], -512.0))
-    done("v", V.memset(T.zz[:, 0:16], 0.0))
+    done("v", V.memset(T.ut[:, 16:520], 0.0))
+    done("v", V.memset(T.ut[:, 0:8], 0.0))
+    v_ut = done("v", V.memset(T.uoff[:], 2))
+    done("v", V.memset(T.zz[:], 0.0))
     need("gq", v_mu)
     g_mu = done("gq", g.affine_select(T.mu[:], T.mu[:], [[-1, 128]], A.is_gt, 0.0, 0, 1))
-    p, nn = T.pi[:, 0:1], lambda k: T.nn[:, k:k + 1]
-    a4 = ts(T.p4[:], T.pi[:], 3, None, AND, deps=[g_pi])
-    n1 = ts(nn(0), p, 0x66, None, AND)
-    ab = ts(T.bi[:], T.pi[:, 0:32:2], 4, 0x79, SH, AND)
-    n5 = ts(nn(2), p, 34, None, A.mult)
-    v_off4 = cp(T.off4[:], T.p4[:], [a4])
-    n2 = ts(nn(1), nn(0), 15, 31, A.mult, A.add, [n1])
-    v_boff = cp(T.boff[:], T.bi[:], [ab])
-    ts(nn(5), nn(2), 32, None, AND, deps=[n5])
-    ts(nn(3), nn(1), 1, 16, SH, AND, [n2])
-    ts(nn(4), nn(1), 3, 8, SH, AND)
-    a = ts(nn(6), p, 3, 1, SH, AND)
-    ts(T.nn[:, 8:12], T.pi[:, 0:16:4], 6, 6, SH, AND)
-    ts(nn(12), p, 5, 2, SH, AND)
-    a = tt(T.nn[:, 13:15], T.nn[:, 3:5], T.nn[:, 5:7], A.add, [a])
+    ts(nn(3), nn(0), 0x28, None, AND, deps=[g_pi])
+    ts(nn(4), nn(1), 64, None, AND)
+    ts(nn(5), T.pi[:, 0:1], 4, None, AND)
+    a = ts(nn(6), T.pi[:, 0:1], 4, 4, SH, AND)
+    ts(T.bi[:], T.pi[:], 4, 0xE1, SH, AND)
+    b = ts(nn(2), nn(0), 4, 7, SH, AND)
+    tt(nn(8), nn(3), nn(4), A.add, [a])
+    a = tt(nn(9), nn(5), nn(6), A.not_equal)
+    v_boff = cp(T.boff[:], T.bi[:], [b])
+    v_aco = ts(T.coff[:, 4:5], nn(2), 7, None, A.add)
+    v_nn = tt(nn(7), nn(8), nn(9), A.add, [a])
+    for a, b, base in ((0, 32, -1.0), (32, 64, 0.0), (64, 128, 0.0)):
+        act(T.evw[a:b, 0:M], T.ut[a:b, 16:16 + M], F.Identity, [v_ut], bias=base)
+    act(T.kk[:, 0:1], T.j2[:, 0:1], F.Sign, [g_j2], bias=-111.5)
+    a = act(T.kk[:, 1:2], T.j2[:, 0:1], F.Identity, bias=-48.0)
+    s_kk = act(T.kk[:, 2:3], T.kk[:, 0:1], F.Identity, [a], bias=T.kk[:, 1:2], scale=-64.0)
+
     helpers = _helpers(T, topo, r)
     order = helpers[0][1] + helpers[1][1]
     at = {d: k for k, d in enumerate(order)}
     for k in range(0, N, 2):
-        v_sno = cp(T.snoff[:, 2 * k:2 * k + 4], T.snr[:, 2 * order[k]:2 * order[k] + 4], [d_sn])
-    v_lv = cp(T.lv[:, 8 * r:8 * r + 2], T.snr[:, 2 * r:2 * r + 2])
-    v_nf = tt(T.nf[:], nn(13), nn(14), A.add, [a])
-    v_coff = ts(T.coff[:, 0:5], T.nn[:, 8:13], T.nf[:], None, A.add, deps=[v_nf])
-
-    s_ut = act(T.ut[:], T.uw[:].indirect(T.off4[:]), F.Copy, [v_off4, d_u])
+        v_sno = cp(T.snoff[:, 2 * k:2 * k + 4], T.lv[:, l0 + 2 * order[k]:l0 + 2 * order[k] + 4], [d_sn])
+    need("v", d_u, v_ut)
+    v_uq = done("v", V.quantize_mx(T.uq[:], T.us[:], T.ut[:]))
+    s_rq = act(T.rs[:], T.us[:].indirect(T.uoff[:]), F.Copy, [v_uq])
 
     need("v", d_x)
     v_xq = done("v", V.quantize_mx(T.xq[:], T.xs[:], T.xt[:]))
-    need("v", s_ut)
-    v_uq = done("v", V.quantize_mx(T.uq[:], T.us[:], T.ut[:]))
+    v_rq = cp(words(T.rq[:]), words(T.uq[:]).indirect(T.uoff[:]), [v_uq])
     v_sl = cp(words(T.slq[:]), words(T.xq[:]).indirect(T.snoff[:, 0:16]), [v_xq, v_sno])
+    ts(T.coff[:, 0:1], nn(7), 4, None, A.add, deps=[v_nn])
+    ts(T.coff[:, 1:2], nn(7), 20, None, A.add)
+    ts(T.coff[0:64, 2:3], T.nn[0:64, 7:8], 4, None, A.add)
+    v_coff = ts(T.coff[64:128, 2:3], T.nn[64:128, 7:8], 20, None, A.add)
     s_sl = act(T.sls[:], T.xs[:].indirect(T.snoff[:, 0:16]), F.Copy, [v_xq, v_sno])
     o = CAPP * r
 
-    el, ec, eh = _engines(T, topo, r)
+    el, ec, eh, eq = _engines(T, topo, r)
     need("gq", d_sn)
-    tr = [_transfer(topo, T.cores[d], e, T.snr[:, 2 * d:2 * d + 2], T.lv[:, 8 * r:8 * r + 2], sem.larr) for d, e in el.items()]
-    g.remote_dma_fused(tr, local_sem=sem.loc)
-    g_j2 = done("gq", g.iota(T.j2[:], [[128, 8]], 0, 1, allow_small_or_imprecise_dtypes=True))
+    for call in el:
+        tr = [_transfer(topo, T.cores[d], e, T.lv[:, l0 + 2 * d:l0 + 2 * d + 2], T.lv[:, o:o + 2], sem.larr) for d, e in call.items()]
+        g.remote_dma_fused(tr, local_sem=sem.loc)
     need("gq", s_sl)
-    tr = [_transfer(topo, c, eh[4 * h:4 * h + 4], T.sls[:, 128 * h:128 * h + 128], T.hs[:], sem.harr) for h, (c, _) in enumerate(helpers)]
+    tr = [_transfer(topo, c, eh[h], T.sls[:, 128 * h:128 * h + 128], T.hs[:], sem.harr) for h, (c, _) in enumerate(helpers)]
     g.remote_dma_fused(tr, local_sem=sem.loc)
     need("gq", v_sl)
-    tr = [_transfer(topo, T.cores[d], e, T.slq[:, CAPP * at[d]:CAPP * at[d] + CAPP].bitcast(dt.uint8), T.land[:, o:o + CAPP].bitcast(dt.uint8), sem.arrc)
-          for d, e in ec.items()]
+    slots = lambda d: T.slq[:, CAPP * at[d]:CAPP * at[d] + CAPP].bitcast(dt.uint8)
+    tr = [_transfer(topo, T.cores[d], e, slots(d), T.land[:, o:o + CAPP].bitcast(dt.uint8), sem.arrc) for d, e in ec.items()]
+    tr += [_transfer(topo, helpers[0][0], e, slots(d), T.hq[:, CAPP * k:CAPP * k + CAPP].bitcast(dt.uint8), sem.harq) for k, (d, e) in enumerate(eq.items())]
     g.remote_dma_fused(tr, local_sem=sem.loc)
-    local = sum(len(e) for e in el.values()) + sum(len(e) for e in ec.values()) + len(eh)
-    larr, arrc = [(nm, sum(len(_engines(T, topo, s)[i][r]) for s in range(N) if s != r)) for i, nm in enumerate(("larr", "arrc"))]
+    local = sum(len(e) for call in el + [ec, eq] for e in call.values()) + sum(len(e) for e in eh)
+    larr = ("larr", sum(len(call.get(r, [])) for s in range(N) for call in _engines(T, topo, s)[0]))
+    arrc = ("arrc", sum(len(_engines(T, topo, s)[1].get(r) or _hand_on(topo, T, s, 0)[r]) for s in range(N) if s != r))
     arrs = ("arrs", sum(len(_hand_on(topo, T, s, h).get(r, [])) for s in range(N) for h in range(2)))
-    v_zr = done("gq", g.iota(T.zr[:], [[0, NS]], 0, 0, allow_small_or_imprecise_dtypes=True))
-    g_ev = done("gq", g.iota(T.evin[0:32, :], [[1, 256]], 0, 0, allow_small_or_imprecise_dtypes=True))
-    need("gq", g_ev)
-    g_ev = done("gq", g.iota(T.evin[64:96, :], [[1, 256]], 257, 0, allow_small_or_imprecise_dtypes=True))
+    g_ev = g_mu
+    for a, base in ((0, 0), (64, 257)):
+        need("gq", g_ev)
+        g_ev = fill(T.evin[a:a + 32, :], [[1, 256]], base, 0)
 
-    need("t", v_uq)
-    t_pc, t_r, t_s = {}, {}, {}
+    t_c, t_r = {}, {}
 
     def row(nm, h):
         a = C + 256 * h
-        return done("t", g.tensor.matmul_mx(T[nm + "ac"[h]][:, 0:256], T.uq[:], T.us[:], T.cand[:, a:a + 256],
-                                            T.cands[:, a:a + 256], True, True))
+        t_r[nm, h] = done("t", g.tensor.matmul_mx(T[nm + str(h)][:, 0:256], T.rq[:], T.rs[:], T.cand[:, a:a + 256], T.cands[:, a:a + 256], True, True))
 
-    def col(k):
-        a = C + 128 * k
-        t_pc[k] = done("t", g.tensor.matmul_mx(T["pc%d" % k][:, 0:128], T.cand[:, a:a + 128], T.cands[:, a:a + 128], T.uq[:], T.us[:], True, True))
+    def col(nm, h):
+        for j in range(2):
+            a, b = C + 256 * h + 128 * j, 2 - 2 * j
+            t_c[nm, h] = done("t", g.tensor.matmul_mx(T[nm + str(h)][:, 0:128], T.cand[:, a:a + 128], T.cands[:, a:a + 128],
+                                                      T.uq[:, b:b + 128], T.us[:, b:b + 128], j == 0, j == 1))
 
-    need("t", d_k[0])
-    col(1)
-    col(0)
-    t_r[0] = row("r", 0)
+    need("t", v_uq, d_k[0])
+    col("cv", 0)
+    need("t", v_rq, s_rq)
+    row("r", 0)
     need("t", d_k[1])
-    t_r[1] = row("r", 1)
-    col(2)
-    col(3)
-    for h in (1, 0):
-        t_s[h] = row("s", h)
+    col("cv", 1)
+    row("r", 1)
+    row("s", 1)
+    row("s", 0)
 
-    v_sv, s_x, s_dl, s_acc, s_ev, v_cm, v_sc = {}, {}, {}, {}, {}, {}, {}
-    for k in (1, 0):
-        v_sv[k] = cp(T.sv[:, k:k + 1], T["pc%d" % k][:, 0:1], [t_pc[k]])
+    s_sv, s_dl, s_x, s_ev, s_acc, v_cm, v_sc = {}, {}, {}, {}, {}, {}, {}
 
     def step(h):
-        s_dl[h] = act(T.dl[:, 2 * h:2 * h + 2], T.sv[:, 2 * h:2 * h + 2], F.Abs, [v_sv[2 * h], v_sv[2 * h + 1], g_mu],
-                      scale=0.74 * 2.0 ** -23, bias=2e-38)
+        s_sv[h] = act(T.sv[:, 2 * h:2 * h + 2], T["cv%d" % h][:, 0:4:2], F.Copy, [t_c["cv", h]])
+        s_dl[h] = act(T.dl[:, 2 * h:2 * h + 2], T["cv%d" % h][:, 0:4:2], F.Abs, scale=0.74 * 2.0 ** -23, bias=2e-38)
 
     def threshold(k):
-        s_x[k] = act(T.xx[:, 128 * k:128 * k + 128], T.mu[:], F.Identity, [s_dl[k // 2]], bias=T.sv[:, k:k + 1], scale=T.dl[:, k:k + 1])
+        s_x[k] = act(T.xx[:, 128 * k:128 * k + 128], T.mu[:], F.Identity, [s_dl[k // 2], g_mu], bias=T.sv[:, k:k + 1], scale=T.dl[:, k:k + 1])
+
+    def scores(h):
+        s_ev[h] = act(T.evin[32 + 64 * h:64 + 64 * h, :], T["s%d" % h][32 + 64 * h:64 + 64 * h, 0:256], F.Copy, [t_r["s", h]])
+
+    def outer(k, h, lo, hi, op):
+        v_cm[k] = ts(T.cm[:, 512 * k + 256 * h + lo:512 * k + 256 * h + hi], T["r%d" % h][:, lo:hi],
+                     T.sv[:, k:k + 1], None, op, deps=[t_r["r", h], s_sv[k // 2]])
+
+    def inner(k):
+        a = 128 * (k % 2)
+        v_cm[k] = tt(T.cm[:, 640 * k:640 * k + 128], T["r%d" % (k // 2)][:, a:a + 128], T.xx[:, 128 * k:128 * k + 128], A.is_lt, [s_x[k]])
+
+    def total(k, first=0.0, deps=()):
+        n = 128 if deps else 256
+        need("v", v_cm[k], *deps)
+        a = 2048 - 8 * n + 2 * (k ^ 1) + 1
+        v_sc[k] = done("v", V.tensor_tensor_scan(T.scl[:, a:2048:8], T.cm[:, 512 * k:512 * k + n], T.cm[:, 512 * k + n:512 * k + 2 * n], first, A.add, A.add))
 
     def signs(k):
-        s_acc[k] = act(T.sg[:, 256 * k:256 * k + 256], T.sc[:, 0:256], F.Sign, [t_s[1], v_sv[k]], bias=T.sv[:, k:k + 1], scale=-1.0)
+        s_acc[k] = act(T.sg[:, 256 * k:256 * k + 256], T.s1[:, 0:256], F.Sign, [t_r["s", 1], s_sv[0]], bias=T.sv[:, k:k + 1], scale=-1.0)
 
     def below(k):
         s_acc[k] = act(T.jk[:, 256 * k:256 * k + 256], T.sg[:, 256 * k:256 * k + 256], F.Relu, [s_acc[k]], accum_out=T.acc[:, k:k + 1])
 
-    def column(k):
-        v_sv[k] = act(T.sv[:, k:k + 1], T["pc%d" % k][:, 0:1], F.Copy, [t_pc[k]])
-
-    def scores(h):
-        s_ev[h] = act(T.evin[32 + 64 * h:64 + 64 * h, :], T["s" + "ac"[h]][32 + 64 * h:64 + 64 * h, 0:256], F.Copy, [t_s[h]])
-
-    def outer(k, h, lo, hi, op):
-        v_cm[k] = ts(T.cm[:, 512 * k + 256 * h + lo:512 * k + 256 * h + hi], T["r" + "ac"[h]][:, lo:hi],
-                     T.sv[:, k:k + 1], None, op, deps=[t_r[h], v_sv[k]])
-
-    def inner(k):
-        a = 128 * (k % 2)
-        v_cm[k] = tt(T.cm[:, 640 * k:640 * k + 128], T["r" + "ac"[k // 2]][:, a:a + 128], T.xx[:, 128 * k:128 * k + 128], A.is_lt,
-                     [s_x[k], t_r[k // 2]])
-
-    def total(k):
-        n, first = (128, T.acc[:, k:k + 1]) if k in s_acc else (256, 0.0)
-        need("v", v_cm[k], *([s_acc[k]] if k in s_acc else []))
-        v_sc[k] = done("v", V.tensor_tensor_scan(T.scl[:, 256 * k + 256 - n:256 * k + 256], T.cm[:, 512 * k:512 * k + n],
-                                                 T.cm[:, 512 * k + n:512 * k + 2 * n], first, A.add, A.add))
-
-    def stay(k):
-        return ts(T.w8[:, k:k + 1], T.scl[:, 256 * k + 255:256 * k + 256], T.pre[:, 255:256], T.j2[:, 4 + k:5 + k], A.is_ge, A.mult,
-                  [v_sc[k], v_pre, g_j2])
-
     step(0)
-    outer(1, 0, 0, 128, A.is_le)
-    outer(0, 0, 128, 256, A.is_lt)
-    column(2)
-    column(3)
     threshold(0)
     step(1)
-    for k in (1, 2, 3):
-        threshold(k)
-    s_bc = act(T.bc[:], T.lv[:].indirect(T.boff[:]), F.Sign, [larr, v_lv, v_boff], bias=1.0)
+    threshold(1)
+    threshold(2)
+    threshold(3)
+    signs(0)
     signs(1)
+    s_bc = act(T.bc[:], T.lv[:].indirect(T.boff[:]), F.Sign, [larr, d_sn, v_boff], bias=1.0)
+    below(0)
     below(1)
-    scores(0)
-    outer(0, 1, 0, 256, A.is_lt)
-    outer(2, 1, 128, 256, A.is_lt)
-    outer(2, 0, 0, 256, A.is_le)
-    inner(0)
-    outer(3, 0, 0, 256, A.is_le)
-    for k in (2, 3, 1):
-        inner(k)
-    total(0)
-    need("v", s_bc)
-    v_vr = done("v", V.transpose(T.vrow[:], T.bc[:]))
-    outer(3, 1, 0, 128, A.is_le)
-    total(2)
-    need("v", v_vr, v_zr)
-    v_pre = done("v", V.tensor_tensor_scan(T.pre[:], T.vrow[:], T.zr[:], -0.5, A.add, A.add))
-    s_a = act(T.jk[:, 512:767], T.pre[:, 0:255], F.Sign, [v_pre, g_j2], bias=T.j2[:, 0:1], scale=-1.0, accum_out=T.w8[:, 4:5])
-    s_own = act(T.lands[:, o:o + CAPP], T.xs[:].indirect(T.snoff[:, 2 * at[r]:2 * at[r] + 2]), F.Copy)
-    total(3)
-    total(1)
-    for k in (0, 2, 3, 1):
-        v_w8 = stay(k)
-
-    tt(T.zz[:, 0:5], T.scl[:, 255:1280:256], T.w8[:, 0:5], A.max, [s_a, v_w8])
-    for h in range(2):
-        a, b = 64 * h, 64 - 64 * h
-        v_ab = tt(T.zz[a:a + 64, 8:13], T.scl[b:b + 64, 255:1280:256], T.w8[b:b + 64, 0:5], A.max)
-    v_own = cp(words(T.land[:, o:o + CAPP]), words(T.xq[:]).indirect(T.snoff[:, 2 * at[r]:2 * at[r] + 2]))
-    for q in range(2):
-        a, b = 32 * q, 32 * q + 32
-        v_zb = cp(T.zz[a:a + 32, 16:32], T.zz[b:b + 32, 0:16], [v_ab])
-        a, b = 64 + a, (64 + b) % 128
-        s_zb = act(T.zz[a:a + 32, 16:32], T.zz[b:b + 32, 0:16], F.Copy, [v_ab])
-    scores(1)
+    outer(1, 0, 0, 128, A.is_le)
+    outer(0, 0, 128, 256, A.is_lt)
     need("v", d_w)
     v_wq = done("v", V.quantize_mx(T.wq[:], T.ws[:], T.wt[:]))
-    need("v", v_zb, s_zb)
+    outer(2, 0, 0, 256, A.is_le)
+    outer(3, 0, 0, 256, A.is_le)
+    inner(0)
+    outer(3, 1, 0, 128, A.is_le)
+    inner(1)
+    outer(2, 1, 128, 256, A.is_lt)
+    inner(2)
+    inner(3)
+    total(2)
+    v_vr = turn(T.vrow[:], T.bc[:], [s_bc])
+    total(3)
+    own = T.snoff[:, 2 * at[r]:2 * at[r] + 2]
+    v_own = cp(words(T.land[:, o:o + CAPP]), words(T.xq[:]).indirect(own))
+    s_own = act(T.lands[:, o:o + CAPP], T.xs[:].indirect(own), F.Copy)
+    need("v", v_vr)
+    v_pre = done("v", V.tensor_tensor_scan(T.pre[:, 2:2 + NS], T.vrow[:], T.ut[:, 16:16 + NS], -0.5, A.add, A.add))
+    total(0, T.acc[:, 0:1], [s_acc[0]])
+    total(1, T.acc[:, 1:2], [s_acc[1]])
+
+    for j in range(2):
+        v_a = s_a = act(T.jk[:, 512 + 256 * j:767 + 256 * j], T.pre[:, 2:257], F.Sign, [v_pre, s_kk], bias=T.kk[:, 2:3] if j else T.j2[:, 0:1],
+                        scale=-1.0, accum_out=T.a2[:, 127 + j:128 + j])
+    v_w8 = ts(T.scl[:, 2040:2048:2], T.scl[:, 2041:2048:2], T.pre[:, 257:258], 2048.0, A.is_ge, A.mult, [v_sc[1], v_pre, g_j2])
+
+    need("v", v_w8)
+    for x, a, b, n in ((0, 0, 0, 128), (1, 0, 64, 64), (1, 64, 0, 64)):
+        v_ab = done("v", V.tensor_tensor_scan(T.zz[a:a + n, x:32:4], T.j2[b:b + n, 8:16], T.scl[b:b + n, 2040:2048], 0.0, A.min, A.max))
+    for q in range(2):
+        a, b = 32 * q, 32 * q + 32
+        v_b = cp(T.a2[a:a + 32, 129:131], T.a2[b:b + 32, 127:129], [s_a, v_a])
+        a, b = 64 + a, (64 + b) % 128
+        s_b = act(T.a2[a:a + 32, 129:131], T.a2[b:b + 32, 127:129], F.Copy, [s_a, v_a])
     for h in range(2):
-        v_zt = done("v", V.transpose(T.zt[:, 32 * h:32 * h + 32], T.zz[:, 0:32]))
-    done("v", V.memset(T.evw[:, 0:M], 0.0))
-    need("v", v_zt)
-    v_sw = done("v", V.transpose(T.zz[:, 32:64], T.zt[:, 16:48]))
-    need("v", (v_sw[0], v_sw[1] - 1))
-    v_evw = done("v", V.memset(T.evw[0:32, 0:M], -1.0))
-    v_ao = ts(T.aoff[:], T.zz[:].indirect(T.coff[:, 2:3]), 0.5, 127.5, A.mult, A.add, [v_sw, v_coff])
-    v_fo = cp(T.foff[:], T.zz[:].indirect(T.coff[:, 0:2]))
-    v_eo = cp(T.eoff[:], T.zz[:].indirect(T.coff[:, 4:5]))
+        a, b = 64 * h, 64 - 64 * h
+        s_c = act(T.a2[a:a + 64, 131:135], T.a2[b:b + 64, 127:131], F.Copy, [s_b, v_b])
+    scores(0)
+    scores(1)
+    turn(T.zt[:, 0:32], T.zz[:], [v_ab])
+    turn(T.zt[:, 64:96], T.zz[:])
+    for q in range(4):
+        a, b = 32 * q, 32 * (q ^ 1)
+        v_zt = turn(T.zt[a:a + 32, 32:64], T.zz[b:b + 32, :])
+    v_ao = ts(T.aoff[:], T.a2[:, 120:136].indirect(T.coff[:, 4:5]), 0.5, 127.5, A.mult, A.add, [s_c, v_aco])
+    turn(T.zu[:, 0:64], T.zt[:, 0:64], [v_zt])
+    v_sw = turn(T.zu[:, 64:128], T.zt[:, 16:80])
     v_arr = cp(words(T.cand[:, 0:M]), words(T.land[:]).indirect(T.aoff[:, 0:8]), [v_ao, arrc, v_own])
     s_arr = act(T.cands[:, 0:M], T.lands[:].indirect(T.aoff[:, 0:8]), F.Copy, [v_ao, arrs, s_own])
+    v_fo = cp(T.foff[:], T.zu[:].indirect(T.coff[:, 0:3]), [v_sw, v_coff])
 
     need("v", v_fo, v_arr, d_k[0], d_k[1])
     need("s", v_fo, s_arr, d_k[0], d_k[1])
     v_af, s_af, t_y = [], [], []
-    for k in range(2):
-        a, f = 256 * k, T.foff[:, 16 * k:16 * k + 16]
-        v_af.append(cp(words(T.aft[:, a:a + 256]), words(T.cand[:]).indirect(f)))
-        s_af.append(act(T.afts[:, a:a + 256], T.cands[:].indirect(f), F.Copy))
+    pieces = [(0, 256, T.cv0), (256, 512, T.cv1)]
+    for k, (a, b, bank) in enumerate(pieces):
+        f = T.foff[:, a // 16:b // 16]
+        v_af.append(cp(words(T.aft[:, a:b]), words(T.cand[:]).indirect(f)))
+        s_af.append(act(T.afts[:, a:b], T.cands[:].indirect(f), F.Copy))
         need("t", v_af[k], s_af[k], v_wq)
-        t_y.append(done("t", g.tensor.matmul_mx(T["pc%d" % k][:, 0:256], T.wq[:], T.ws[:], T.aft[:, a:a + 256], T.afts[:, a:a + 256], True, True)))
+        t_y.append(done("t", g.tensor.matmul_mx(bank[:, 0:b - a], T.wq[:], T.ws[:], T.aft[:, a:b], T.afts[:, a:b], True, True)))
         need("y", v_af[k])
-        load(Y, "d_out", T.oc[:, 4 * a:4 * a + 1024], T.aft[:, a:a + 256].bitcast(dt.uint8))
-    for k in range(2):
-        a = 256 * k
-        s_y = act(T.ysb[:, a:a + 256], T["pc%d" % k][:, 0:256], F.Copy, [t_y[k]])
-        need("s" if k else "y", s_y)
-        load(S if k else Y, "d_out", T.y[:, a:a + 256], T.ysb[:, a:a + 256])
-    a = cp(T.evw[:].indirect(T.eoff[:]), T.evin[:], [v_eo, s_ev[1], g_ev, v_evw])
-    v_ev = tt(T.evo[0:64, :], T.evw[0:64, 0:M], T.evw[64:128, 0:M], A.add, [a])
-    need("y", s_af[1])
+        load(Y, "d_out", T.oc[:, 4 * a:4 * b], T.aft[:, a:b].bitcast(dt.uint8))
+    need("y", s_af[-1])
     for k in range(4):
-        d_out = load(Y, "d_out", T.osc[4 * k:4 * k + 4, :], T.afts[32 * k:32 * k + 4, :])
+        load(Y, "d_out", T.osc[4 * k:4 * k + 4, :], T.afts[32 * k:32 * k + 4, :])
+    for k, (a, b, bank) in enumerate(pieces):
+        s_y = act(T.ysb[:, a:b], bank[:, 0:b - a], F.Copy, [t_y[k]])
+        need("s" if k else "y", s_y)
+        d_out = load(S if k else Y, "d_out", T.y[:, a:b], T.ysb[:, a:b])
+    a = cp(T.evw[:].indirect(T.foff[:, 32:48]), T.evin[:], [s_ev[1], g_ev])
+    v_ev = tt(T.evo[0:64, :], T.evw[0:64, 0:M], T.evw[64:128, 0:M], A.add, [a])
     need("y", v_ev)
     need("s", v_ev)
     load(Y, "d_ev", T.ev[0:1, :], T.evo[0:1, :])

from concourse.bass import DstId, RemoteDMATransfer
from concourse.mybir import dt, AluOpType as A, ActivationFunctionType as F

N, CAPP, C, M = 8, 32, 512, 128
NS = N * CAPP
X4, U8, F32, BF, I32, U16 = "float8_e4m3fn_x4", "uint8", "float32", "bfloat16", "int32", "uint16"


def _sb(n, d):
    return ("sbuf", [128, n], d)


SCRATCH = {
    "lv": _sb(256, I32), "snoff": _sb(16, U16),
    "xt": _sb(1024, BF), "xq": _sb(256, X4), "xs": _sb(256, U8),
    "slq": _sb(256, X4), "sls": _sb(256, U8), "hs": _sb(128, U8), "hq": _sb(64, X4), "land": _sb(NS, X4), "lands": _sb(NS, U8),
    "cand": _sb(2 * C, X4), "cands": _sb(2 * C, U8), "aft": _sb(512, X4), "afts": _sb(512, U8),
    "ut": _sb(520, BF), "uq": _sb(130, X4), "us": _sb(130, U8), "uoff": _sb(8, U16), "rq": _sb(128, X4), "rs": _sb(128, U8),
    "wt": _sb(512, BF), "wq": _sb(128, X4), "ws": _sb(128, U8),
    "pi": _sb(16, I32), "bi": _sb(16, I32), "boff": _sb(16, U16), "nn": _sb(16, I32), "coff": _sb(6, U16),
    "mu": _sb(128, F32), "j2": _sb(16, F32), "kk": _sb(4, F32),
    "bc": _sb(256, BF), "vrow": _sb(256, BF), "pre": _sb(258, BF),
    "sv": _sb(4, F32), "dl": _sb(4, F32), "xx": _sb(512, F32), "cm": _sb(2048, BF), "scl": _sb(2048, BF), "jk": _sb(1024, BF),
    "sg": _sb(512, BF), "acc": _sb(2, F32), "a2": _sb(136, F32), "zz": _sb(32, F32), "zt": _sb(96, F32), "zu": _sb(128, F32),
    "aoff": _sb(16, U16), "foff": _sb(48, U16),
    "evin": _sb(256, F32), "evw": _sb(1024, F32), "evo": _sb(128, F32), "ysb": _sb(512, F32),
}
for _n in ("r0", "r1", "s0", "s1", "cv0", "cv1"):
    SCRATCH[_n] = ("psum", [128, 512], F32)
SEMAPHORES = ["v", "s", "t", "gq", "d_sn", "d_x", "d_u", "d_k0", "d_k1", "d_w", "d_ev", "d_out", "larr", "arrc", "arrs", "harr", "harq", "loc"]


def _share(dst, engs):
    w = len(engs) // len(dst)
    return {d: engs[w * k:w * k + w] for k, d in enumerate(dst)}


def _engines(T, topo, s):
    me = T.cores[s]
    rest = [(s + k) % N for k in range(1, N)]
    on = [d for d in rest if topo.chip(T.cores[d]) == topo.chip(me)]
    off = [d for d in rest if topo.chip(T.cores[d]) != topo.chip(me)]
    e_off = topo.engines(me, T.cores[off[0]])
    e_on = [e for e in topo.engines(me, T.cores[on[0]]) if e not in e_off]
    (_, mine), (_, others) = _helpers(T, topo, s)
    lists = [{**_share(off[:4], e_off[0::2]), **_share(off[4:], e_off[1::2])}]
    codes = {**_share(off[2:], e_off[1::2]), **_share(off[:2], e_off[0::2])}
    lists[0][on[0]], codes[on[0]] = e_on[:2], e_on[:4]
    return lists, codes, [e_on[:4], e_on[4:]], {}


def _helpers(T, topo, s):
    me = T.cores[s]
    idle = [c for c in topo.cores_of(me) if c not in T.cores and topo.die(c) != topo.die(me)]
    k = [c for c in topo.cores_of(me) if c in T.cores].index(me)
    far = [c for c in idle if all(topo.may_write(c, d) for d in T.cores)]
    mid = [c for c in idle if c not in far][k]
    mine = [d for d in range(N) if topo.may_write(mid, T.cores[d])]
    return [(mid, mine), (far[k], [d for d in range(N) if d not in mine])]


def _hand_on(topo, T, s, h):
    core, dst = _helpers(T, topo, s)[h]
    off = [d for d in dst if topo.chip(T.cores[d]) != topo.chip(core)]
    e_off = topo.engines(core, T.cores[off[0]])
    r = _share(off, e_off)
    for d in dst:
        if d not in off and d != s:
            r[d] = [e for e in topo.engines(core, T.cores[d]) if e not in e_off][:2]
    return r


def _transfer(topo, core, engs, src, dst, sem):
    rid, pid, _ = topo.addr(core)
    return RemoteDMATransfer(dst_ids=[DstId(rid=rid, pnc=pid)], dma_engine_mask=sum(1 << e for e in engs), remote_sem=sem, srcs=[src], dsts=[dst])


def helper_program(g, core, T, topo):
    for s in range(N):
        for h, (c, dst) in enumerate(_helpers(T, topo, s)):
            if c == core:
                engs = _hand_on(topo, T, s, h)
                g.wait_ge(T.sem.harr, len(_engines(T, topo, s)[2][h]))
                g.remote_dma_fused([_transfer(topo, T.cores[d], e, T.hs[:, CAPP * dst.index(d):CAPP * dst.index(d) + CAPP],
                                              T.lands[:, CAPP * s:CAPP * s + CAPP], T.sem.arrs) for d, e in engs.items()], local_sem=T.sem.loc)
                local = sum(len(e) for e in engs.values())
                if h == 0 and _engines(T, topo, s)[3]:
                    far = _engines(T, topo, s)[3]
                    g.wait_ge(T.sem.harq, sum(len(e) for e in far.values()))
                    g.remote_dma_fused([_transfer(topo, T.cores[d], engs[d], T.hq[:, CAPP * k:CAPP * k + CAPP].bitcast(dt.uint8),
                                                  T.land[:, CAPP * s:CAPP * s + CAPP].bitcast(dt.uint8), T.sem.arrc) for k, d in enumerate(far)],
                                       local_sem=T.sem.loc)
                    local += sum(len(engs[d]) for d in far)
                g.wait_ge(T.sem.loc, local)


def rank_program(g, core, T, topo):
    r = T.rank_of(core)
    if r is None:
        return helper_program(g, core, T, topo)
    sem = T.sem
    cnt = {"v": 0, "s": 0, "t": 0, "gq": 0}
    seen = {}
    qs = {"v": g.vector, "s": g.scalar, "t": g.tensor, "gq": g, "y": g.sync}

    def need(q, *deps):
        for name, val in deps:
            if seen.get((q, name), 0) < val:
                qs[q].wait_ge(sem[name], val)
                seen[(q, name)] = val

    def done(q, ins):
        ins.then_inc(sem[q], 1)
        cnt[q] += 1
        return (q, cnt[q])

    V, S, Y = g.vector, g.scalar, g.sync
    dma = {}

    def load(q, name, out, in_):
        q.dma_start(out, in_).then_inc(sem[name], 16)
        dma[name] = dma.get(name, 0) + 16
        return (name, dma[name])

    def ts(out, in0, a, b, op0, op1=None, deps=()):
        need("v", *deps)
        if op1 is None:
            return done("v", V.tensor_scalar(out, in0, a, None, op0))
        return done("v", V.tensor_scalar(out, in0, a, b, op0, op1))

    def tt(out, in0, in1, op, deps=()):
        need("v", *deps)
        return done("v", V.tensor_tensor(out, in0, in1, op))

    def cp(out, in_, deps=()):
        need("v", *deps)
        return done("v", V.tensor_copy(out, in_))

    def turn(out, in_, deps=()):
        need("v", *deps)
        return done("v", V.transpose(out, in_))

    def act(out, in_, func, deps=(), **kw):
        need("s", *deps)
        return done("s", S.activation(out, in_, func, **kw))

    def fill(out, pattern, base, step):
        return done("gq", g.iota(out, pattern, base, step, allow_small_or_imprecise_dtypes=True))

    def words(ap):
        return ap.bitcast(dt.uint32)

    l0 = 30 * r
    for k in range(4):
        load(Y, "d_sn", T.lv[16 * k:16 * k + 16, l0:l0 + 16], T.sn[:])
        d_sn = load(S, "d_sn", T.lv[64 + 16 * k:80 + 16 * k, l0:l0 + 16], T.sn[:])
    d_u = load(S, "d_u", T.ut[:, 8:16], T.u[:, 0:8])
    d_x = load(Y, "d_x", T.xt[:], T.x[:])
    d_k = []
    for k in range(2):
        a, b = 256 * k, 256 * k + 256
        load(Y, "d_k%d" % k, T.cand[:, C + a:C + b].bitcast(dt.uint8), T.kc[:, 4 * a:4 * b])
        d_k.append(load(Y, "d_k%d" % k, T.cands[:, C + a:C + b], T.ks[:, a:b]))
    d_w = load(Y, "d_w", T.wt[:], T.w[:])

    SH, AND = A.arith_shift_right, A.bitwise_and
    nn = lambda k: T.nn[:, k:k + 1]
    done("gq", g.iota(T.pi[:], [[512, 8], [0, 2]], 0, 1))
    done("gq", g.iota(nn(0), [[0, 1]], 15, 15))
    g_pi = done("gq", g.iota(nn(1), [[0, 1]], 0, 68))
    fill(T.j2[:, 0:1], [[0, 1]], 0, 1)
    g_j2 = fill(T.j2[:, 8:16], [[256, 2], [-128, 2], [4096, 2]], C + 128 - 4096, 1)
    v_mu = done("v", V.memset(T.mu[:], 1.0))
    done("v", V.memset(T.ut[:, 16:520], 0.0))
    done("v", V.memset(T.ut[:, 0:8], 0.0))
    v_ut = done("v", V.memset(T.uoff[:], 2))
    done("v", V.memset(T.zz[:], 0.0))
    need("gq", v_mu)
    g_mu = done("gq", g.affine_select(T.mu[:], T.mu[:], [[-1, 128]], A.is_gt, 0.0, 0, 1))
    ts(nn(3), nn(0), 0x28, None, AND, deps=[g_pi])
    ts(nn(4), nn(1), 64, None, AND)
    ts(nn(5), T.pi[:, 0:1], 4, None, AND)
    a = ts(nn(6), T.pi[:, 0:1], 4, 4, SH, AND)
    ts(T.bi[:], T.pi[:], 4, 0xE1, SH, AND)
    b = ts(nn(2), nn(0), 4, 7, SH, AND)
    tt(nn(8), nn(3), nn(4), A.add, [a])
    a = tt(nn(9), nn(5), nn(6), A.not_equal)
    v_boff = cp(T.boff[:], T.bi[:], [b])
    v_aco = ts(T.coff[:, 4:5], nn(2), 7, None, A.add)
    v_nn = tt(nn(7), nn(8), nn(9), A.add, [a])
    for a, b, base in ((0, 32, -1.0), (32, 64, 0.0), (64, 128, 0.0)):
        act(T.evw[a:b, 0:M], T.ut[a:b, 16:16 + M], F.Identity, [v_ut], bias=base)
    act(T.kk[:, 0:1], T.j2[:, 0:1], F.Sign, [g_j2], bias=-111.5)
    a = act(T.kk[:, 1:2], T.j2[:, 0:1], F.Identity, bias=-48.0)
    s_kk = act(T.kk[:, 2:3], T.kk[:, 0:1], F.Identity, [a], bias=T.kk[:, 1:2], scale=-64.0)

    helpers = _helpers(T, topo, r)
    order = helpers[0][1] + helpers[1][1]
    at = {d: k for k, d in enumerate(order)}
    for k in range(0, N, 2):
        v_sno = cp(T.snoff[:, 2 * k:2 * k + 4], T.lv[:, l0 + 2 * order[k]:l0 + 2 * order[k] + 4], [d_sn])
    need("v", d_u, v_ut)
    v_uq = done("v", V.quantize_mx(T.uq[:], T.us[:], T.ut[:]))
    s_rq = act(T.rs[:], T.us[:].indirect(T.uoff[:]), F.Copy, [v_uq])

    need("v", d_x)
    v_xq = done("v", V.quantize_mx(T.xq[:], T.xs[:], T.xt[:]))
    v_rq = cp(words(T.rq[:]), words(T.uq[:]).indirect(T.uoff[:]), [v_uq])
    v_sl = cp(words(T.slq[:]), words(T.xq[:]).indirect(T.snoff[:, 0:16]), [v_xq, v_sno])
    ts(T.coff[:, 0:1], nn(7), 4, None, A.add, deps=[v_nn])
    ts(T.coff[:, 1:2], nn(7), 20, None, A.add)
    ts(T.coff[0:64, 2:3], T.nn[0:64, 7:8], 4, None, A.add)
    v_coff = ts(T.coff[64:128, 2:3], T.nn[64:128, 7:8], 20, None, A.add)
    s_sl = act(T.sls[:], T.xs[:].indirect(T.snoff[:, 0:16]), F.Copy, [v_xq, v_sno])
    o = CAPP * r

    el, ec, eh, eq = _engines(T, topo, r)
    need("gq", d_sn)
    for call in el:
        tr = [_transfer(topo, T.cores[d], e, T.lv[:, l0 + 2 * d:l0 + 2 * d + 2], T.lv[:, o:o + 2], sem.larr) for d, e in call.items()]
        g.remote_dma_fused(tr, local_sem=sem.loc)
    need("gq", s_sl)
    tr = [_transfer(topo, c, eh[h], T.sls[:, 128 * h:128 * h + 128], T.hs[:], sem.harr) for h, (c, _) in enumerate(helpers)]
    g.remote_dma_fused(tr, local_sem=sem.loc)
    need("gq", v_sl)
    slots = lambda d: T.slq[:, CAPP * at[d]:CAPP * at[d] + CAPP].bitcast(dt.uint8)
    tr = [_transfer(topo, T.cores[d], e, slots(d), T.land[:, o:o + CAPP].bitcast(dt.uint8), sem.arrc) for d, e in ec.items()]
    tr += [_transfer(topo, helpers[0][0], e, slots(d), T.hq[:, CAPP * k:CAPP * k + CAPP].bitcast(dt.uint8), sem.harq) for k, (d, e) in enumerate(eq.items())]
    g.remote_dma_fused(tr, local_sem=sem.loc)
    local = sum(len(e) for call in el + [ec, eq] for e in call.values()) + sum(len(e) for e in eh)
    larr = ("larr", sum(len(call.get(r, [])) for s in range(N) for call in _engines(T, topo, s)[0]))
    arrc = ("arrc", sum(len(_engines(T, topo, s)[1].get(r) or _hand_on(topo, T, s, 0)[r]) for s in range(N) if s != r))
    arrs = ("arrs", sum(len(_hand_on(topo, T, s, h).get(r, [])) for s in range(N) for h in range(2)))
    g_ev = g_mu
    for a, base in ((0, 0), (64, 257)):
        need("gq", g_ev)
        g_ev = fill(T.evin[a:a + 32, :], [[1, 256]], base, 0)

    t_c, t_r = {}, {}

    def row(nm, h):
        a = C + 256 * h
        t_r[nm, h] = done("t", g.tensor.matmul_mx(T[nm + str(h)][:, 0:256], T.rq[:], T.rs[:], T.cand[:, a:a + 256], T.cands[:, a:a + 256], True, True))

    def col(nm, h):
        for j in range(2):
            a, b = C + 256 * h + 128 * j, 2 - 2 * j
            t_c[nm, h] = done("t", g.tensor.matmul_mx(T[nm + str(h)][:, 0:128], T.cand[:, a:a + 128], T.cands[:, a:a + 128],
                                                      T.uq[:, b:b + 128], T.us[:, b:b + 128], j == 0, j == 1))

    need("t", v_uq, d_k[0])
    col("cv", 0)
    need("t", v_rq, s_rq)
    row("r", 0)
    need("t", d_k[1])
    col("cv", 1)
    row("r", 1)
    row("s", 1)
    row("s", 0)

    s_sv, s_dl, s_x, s_ev, s_acc, v_cm, v_sc = {}, {}, {}, {}, {}, {}, {}

    def step(h):
        s_sv[h] = act(T.sv[:, 2 * h:2 * h + 2], T["cv%d" % h][:, 0:4:2], F.Copy, [t_c["cv", h]])
        s_dl[h] = act(T.dl[:, 2 * h:2 * h + 2], T["cv%d" % h][:, 0:4:2], F.Abs, scale=0.74 * 2.0 ** -23, bias=2e-38)

    def threshold(k):
        s_x[k] = act(T.xx[:, 128 * k:128 * k + 128], T.mu[:], F.Identity, [s_dl[k // 2], g_mu], bias=T.sv[:, k:k + 1], scale=T.dl[:, k:k + 1])

    def scores(h):
        s_ev[h] = act(T.evin[32 + 64 * h:64 + 64 * h, :], T["s%d" % h][32 + 64 * h:64 + 64 * h, 0:256], F.Copy, [t_r["s", h]])

    def outer(k, h, lo, hi, op):
        v_cm[k] = ts(T.cm[:, 512 * k + 256 * h + lo:512 * k + 256 * h + hi], T["r%d" % h][:, lo:hi],
                     T.sv[:, k:k + 1], None, op, deps=[t_r["r", h], s_sv[k // 2]])

    def inner(k):
        a = 128 * (k % 2)
        v_cm[k] = tt(T.cm[:, 640 * k:640 * k + 128], T["r%d" % (k // 2)][:, a:a + 128], T.xx[:, 128 * k:128 * k + 128], A.is_lt, [s_x[k]])

    def total(k, first=0.0, deps=()):
        n = 128 if deps else 256
        need("v", v_cm[k], *deps)
        a = 2048 - 8 * n + 2 * (k ^ 1) + 1
        v_sc[k] = done("v", V.tensor_tensor_scan(T.scl[:, a:2048:8], T.cm[:, 512 * k:512 * k + n], T.cm[:, 512 * k + n:512 * k + 2 * n], first, A.add, A.add))

    def signs(k):
        s_acc[k] = act(T.sg[:, 256 * k:256 * k + 256], T.s1[:, 0:256], F.Sign, [t_r["s", 1], s_sv[0]], bias=T.sv[:, k:k + 1], scale=-1.0)

    def below(k):
        s_acc[k] = act(T.jk[:, 256 * k:256 * k + 256], T.sg[:, 256 * k:256 * k + 256], F.Relu, [s_acc[k]], accum_out=T.acc[:, k:k + 1])

    step(0)
    threshold(0)
    step(1)
    threshold(1)
    threshold(2)
    threshold(3)
    signs(0)
    signs(1)
    s_bc = act(T.bc[:], T.lv[:].indirect(T.boff[:]), F.Sign, [larr, d_sn, v_boff], bias=1.0)
    below(0)
    below(1)
    outer(1, 0, 0, 128, A.is_le)
    outer(0, 0, 128, 256, A.is_lt)
    need("v", d_w)
    v_wq = done("v", V.quantize_mx(T.wq[:], T.ws[:], T.wt[:]))
    outer(2, 0, 0, 256, A.is_le)
    outer(3, 0, 0, 256, A.is_le)
    inner(0)
    outer(3, 1, 0, 128, A.is_le)
    inner(1)
    outer(2, 1, 128, 256, A.is_lt)
    inner(2)
    inner(3)
    total(2)
    v_vr = turn(T.vrow[:], T.bc[:], [s_bc])
    total(3)
    own = T.snoff[:, 2 * at[r]:2 * at[r] + 2]
    v_own = cp(words(T.land[:, o:o + CAPP]), words(T.xq[:]).indirect(own))
    s_own = act(T.lands[:, o:o + CAPP], T.xs[:].indirect(own), F.Copy)
    need("v", v_vr)
    v_pre = done("v", V.tensor_tensor_scan(T.pre[:, 2:2 + NS], T.vrow[:], T.ut[:, 16:16 + NS], -0.5, A.add, A.add))
    total(0, T.acc[:, 0:1], [s_acc[0]])
    total(1, T.acc[:, 1:2], [s_acc[1]])

    for j in range(2):
        v_a = s_a = act(T.jk[:, 512 + 256 * j:767 + 256 * j], T.pre[:, 2:257], F.Sign, [v_pre, s_kk], bias=T.kk[:, 2:3] if j else T.j2[:, 0:1],
                        scale=-1.0, accum_out=T.a2[:, 127 + j:128 + j])
    v_w8 = ts(T.scl[:, 2040:2048:2], T.scl[:, 2041:2048:2], T.pre[:, 257:258], 2048.0, A.is_ge, A.mult, [v_sc[1], v_pre, g_j2])

    need("v", v_w8)
    for x, a, b, n in ((0, 0, 0, 128), (1, 0, 64, 64), (1, 64, 0, 64)):
        v_ab = done("v", V.tensor_tensor_scan(T.zz[a:a + n, x:32:4], T.j2[b:b + n, 8:16], T.scl[b:b + n, 2040:2048], 0.0, A.min, A.max))
    for q in range(2):
        a, b = 32 * q, 32 * q + 32
        v_b = cp(T.a2[a:a + 32, 129:131], T.a2[b:b + 32, 127:129], [s_a, v_a])
        a, b = 64 + a, (64 + b) % 128
        s_b = act(T.a2[a:a + 32, 129:131], T.a2[b:b + 32, 127:129], F.Copy, [s_a, v_a])
    for h in range(2):
        a, b = 64 * h, 64 - 64 * h
        s_c = act(T.a2[a:a + 64, 131:135], T.a2[b:b + 64, 127:131], F.Copy, [s_b, v_b])
    scores(0)
    scores(1)
    turn(T.zt[:, 0:32], T.zz[:], [v_ab])
    turn(T.zt[:, 64:96], T.zz[:])
    for q in range(4):
        a, b = 32 * q, 32 * (q ^ 1)
        v_zt = turn(T.zt[a:a + 32, 32:64], T.zz[b:b + 32, :])
    v_ao = ts(T.aoff[:], T.a2[:, 120:136].indirect(T.coff[:, 4:5]), 0.5, 127.5, A.mult, A.add, [s_c, v_aco])
    turn(T.zu[:, 0:64], T.zt[:, 0:64], [v_zt])
    v_sw = turn(T.zu[:, 64:128], T.zt[:, 16:80])
    v_arr = cp(words(T.cand[:, 0:M]), words(T.land[:]).indirect(T.aoff[:, 0:8]), [v_ao, arrc, v_own])
    s_arr = act(T.cands[:, 0:M], T.lands[:].indirect(T.aoff[:, 0:8]), F.Copy, [v_ao, arrs, s_own])
    v_fo = cp(T.foff[:], T.zu[:].indirect(T.coff[:, 0:3]), [v_sw, v_coff])

    need("v", v_fo, v_arr, d_k[0], d_k[1])
    need("s", v_fo, s_arr, d_k[0], d_k[1])
    v_af, s_af, t_y = [], [], []
    pieces = [(0, 256, T.cv0), (256, 512, T.cv1)]
    for k, (a, b, bank) in enumerate(pieces):
        f = T.foff[:, a // 16:b // 16]
        v_af.append(cp(words(T.aft[:, a:b]), words(T.cand[:]).indirect(f)))
        s_af.append(act(T.afts[:, a:b], T.cands[:].indirect(f), F.Copy))
        need("t", v_af[k], s_af[k], v_wq)
        t_y.append(done("t", g.tensor.matmul_mx(bank[:, 0:b - a], T.wq[:], T.ws[:], T.aft[:, a:b], T.afts[:, a:b], True, True)))
        need("y", v_af[k])
        load(Y, "d_out", T.oc[:, 4 * a:4 * b], T.aft[:, a:b].bitcast(dt.uint8))
    need("y", s_af[-1])
    for k in range(4):
        load(Y, "d_out", T.osc[4 * k:4 * k + 4, :], T.afts[32 * k:32 * k + 4, :])
    for k, (a, b, bank) in enumerate(pieces):
        s_y = act(T.ysb[:, a:b], bank[:, 0:b - a], F.Copy, [t_y[k]])
        need("s" if k else "y", s_y)
        d_out = load(S if k else Y, "d_out", T.y[:, a:b], T.ysb[:, a:b])
    a = cp(T.evw[:].indirect(T.foff[:, 32:48]), T.evin[:], [s_ev[1], g_ev])
    v_ev = tt(T.evo[0:64, :], T.evw[0:64, 0:M], T.evw[64:128, 0:M], A.add, [a])
    need("y", v_ev)
    need("s", v_ev)
    load(Y, "d_ev", T.ev[0:1, :], T.evo[0:1, :])
    d_ev = load(S, "d_ev", T.ev[1:2, :], T.evo[32:33, :])

    for n, val in cnt.items():
        need("y", (n, val))
    need("y", d_ev, d_out)
    need("gq", ("loc", local))
